import numpy as np, ml_dtypes
CORES = [2,6,10,14,18,22,26,30]
N = 8
BF = ml_dtypes.bfloat16
W, C, L, H, RO = 4096, 48, 384, 7, 3
ROW = np.arange(16)[:, None]
def parts(rng):
    z = (rng.integers(20, 257, (N, 8, 1, W)) * rng.random((N, 8, 16, W))).astype(np.int64)
    a = 1 + (rng.integers(10, 255, (N, 8, 1, L)) * rng.random((N, 8, 16, L))).astype(np.int64)
    w = rng.integers(0, 16, (N, 8, 16, 1)); e = rng.integers(0, W - 1, (N, 8, 16, L))
    often = np.take_along_axis(rng.integers(0, W - 1, (N, 8, 24)), rng.integers(0, 24, (N, 8, 16 * L)), 2).reshape(e.shape)
    e = np.where(rng.random(e.shape) < 0.1, often, e)
    n = rng.integers(2, 13, (N, 8, 1, L)); u = rng.random(n.shape)
    n = np.where(u < 0.04, 0, np.where(u < 0.07, 1, np.where(u < 0.11, 16, n)))
    return np.where(ROW < n, e, W - 1), a, z, w
def poor(rng, n):
    return np.where(np.argsort(rng.random((16, n)), axis=0) < 17 - H, 0, rng.integers(0, 256, (16, n)))
def pack(e, a, z, w):
    z[..., W - 1] = 0
    return {"bills": np.ascontiguousarray(e.reshape(N, 128, L)).astype(np.int32), "due": np.ascontiguousarray(a.reshape(N, 128, L)).astype(np.float32).astype(BF),
            "z0": np.ascontiguousarray(z.reshape(N, 128, W)).astype(np.float32).astype(BF), "wt": np.ascontiguousarray(w.reshape(N, 128, 1)).astype(np.float32).astype(BF)}
def setup_inputs(rng):
    return pack(*parts(rng))
def setup_inputs_room(rng):
    e, a, z, w = parts(rng); a = rng.integers(1, 41, a.shape); w[:, :, 0] = 1
    for q in range(N):
        for g in range(8):
            o = rng.permutation(W - 1); pay, b = o[:L], o[L:]
            z[q, g][:, b] = poor(rng, len(b)); z[q, g][:, pay] = rng.integers(64, 256, (16, L))
            n = np.full(N, C); d1, d2, d3 = (q + 1) % N, (q + 2) % N, (q + 3) % N
            if g % 4 == 0: n[d2] += 1; n[d3] -= 1
            if g % 4 == 1: n[:] = 0; n[d1] = L
            if g % 4 == 2: n[d1] -= 1; n[q] += 1
            if g % 4 == 3: n[d1] = 0; n[d2] += C
            to = rng.permutation(np.repeat(np.arange(N), n)); k = rng.integers(1, 15, L); top = k + rng.integers(0, 16 - k)
            e[q, g] = np.where(ROW < k, rng.integers(0, W - 1, (16, L)), np.where(ROW == k, pay, np.where(ROW <= top, b[rng.integers(0, len(b), (16, L))], W - 1)))
            s = np.sum(w[q, g] * (z[q, g][:, pay] - a[q, g]), axis=0)
            z[q, g, 0, pay] -= (s - to) % N
    return pack(e, a, z, w)
def setup_inputs_ties(rng):
    e, a, z, w = parts(rng); m = min(8, (W - 1) // L)
    for q in range(N):
        for g in range(8):
            o = rng.permutation(W - 1)[:L * m].reshape(m, L); x = a[q, g][:, None, :]
            n = rng.choice(np.array([0, H - 1, H - 1, H, H, H + 1]), (m, L)); good = np.argsort(rng.random((16, m, L)), axis=0) < n
            u = rng.random((16, m, L)); more = np.where(u < 0.5, 0, np.where(u < 0.65, 1, rng.integers(0, 256, u.shape)))
            if q == 0 and g == 0: more = more * 0
            v = np.where(good, np.minimum(x + more, 255), np.where(rng.random(u.shape) < 0.7, x - 1, 0))
            z[q, g][:, o.reshape(-1)] = v.reshape(16, -1)
            r = ROW - rng.integers(0, 17 - m, L)
            e[q, g] = np.where(r < 0, rng.integers(0, W - 1, (16, L)), np.where(r < m, np.take_along_axis(o, np.clip(r, 0, m - 1), 0), W - 1))
    return pack(e, a, z, w)
def setup_inputs_alike(rng):
    e, a, z, w = parts(rng); a = rng.integers(1, 21, a.shape)
    for q in range(N):
        for g in range(8):
            few = rng.permutation(W - 1)[:(1, 2, 3, 40)[g % 4]]
            if g % 4 == 1: few = np.array([0, W - 2])
            z[q, g][:, few] = rng.integers(160, 256, (16, len(few)))
            e[q, g] = np.where(e[q, g] == W - 1, W - 1, few[rng.integers(0, len(few), (16, L))])
    return pack(e, a, z, w)
def setup_inputs_ends(rng):
    e, a, z, w = parts(rng); a = rng.integers(1, 41, a.shape)
    w[:, 2] = 0; w[:, 3] = 15; w[:, 4] = 0; w[:, 4, :2] = 15; w[:, 4, 2] = 1
    xy = (W - 1) // 15 - 13; left = np.array([xy // 2, xy - xy // 2, W - 1 - 15 * xy])[:, None]; t = L // 4
    for q in range(N):
        for g in range(8):
            o = rng.permutation(W - 1); h, b = o[:W // 2], o[W // 2:]
            z[q, g][:, b] = poor(rng, len(b)); z[q, g][:, h] = rng.integers(128, 256, (16, len(h)))
            ri = h[rng.integers(8, len(h), (16, L))]; po = b[rng.integers(0, len(b), (16, L))]; no = np.full((16, L), W - 1)
            if g == 5:
                z[q, g][:, W - 2] = 200; z[q, g][:, 0] = 150
                u = rng.random((16, L)); ri = np.where(u < 0.1, W - 2, np.where(u < 0.2, 0, ri))
            kind = rng.integers(0, 9, L)[None, :]; some = rng.random((16, L)) < 0.3; one = rng.integers(1, 15, L)
            e[q, g] = np.choose(kind, [no, np.where(ROW == 0, ri, no), ri, np.where(ROW < 15, ri, po), np.where(ROW == 0, ri, po), np.where((ROW % 2 == 0) & (ROW < 14), ri, no),
                                       np.where((ROW > 0) & some, ri, no), np.where(ROW == one, ri, no), np.where((ROW == 15) | (ROW % 4 == 1), ri, no)])
            if g == 0:
                z[q, g][:, h[0]] = 255
                for j in range(2):
                    at = L - 8 + 4 * j; k = int(rng.integers(1, 15))
                    e[q, g][:, at:at + 4] = np.where(ROW < k, ri[:, :1], np.where(ROW == k, h[j], W - 1))
                    a[q, g][:, at:at + 4] = np.full((16, 1), 255) if j == 0 else rng.integers(1, 41, (16, 1))
            if g == 3 or g == 4:
                if g == 3: a[q, g][:, :t] = rng.integers(1, 21, (16, t)); z[q, g][:, h[:t]] = 255
                if g == 4: z[q, g][:3, h[:t]] = a[q, g][:3, :t] + left
                k = rng.integers(1, 15, t)
                e[q, g][:, :t] = np.where(ROW < k, h[rng.integers(t, len(h), (16, t))], np.where(ROW == k, h[:t], W - 1))
    e[:, rng.integers(6, 8)] = W - 1; e[rng.integers(0, N), 1] = W - 1
    return pack(e, a, z, w)
def setup_inputs_spread(rng):
    e, a, z, w = parts(rng)
    z = (np.exp2(8 * rng.random((N, 8, 1, W))) * rng.random(z.shape)).astype(np.int64)
    a = 1 + (np.exp2(7.9 * rng.random((N, 8, 1, L))) * rng.random(a.shape)).astype(np.int64)
    w = (16 * rng.random(w.shape) ** 3).astype(np.int64)
    e = np.where(e == W - 1, W - 1, np.minimum(((W - 1) * rng.random(e.shape) ** 2).astype(np.int64), W - 2))
    return pack(e, a, z, w)
def check_inputs(d):
    bad = []
    for k, lo, hi in (("bills", 0, W - 1), ("due", 1, 255), ("z0", 0, 255), ("wt", 0, 15)):
        v = np.asarray(d[k]).astype(np.float32)
        if not np.all((v >= lo) & (v <= hi) & (v == np.floor(v))): bad.append("range of " + k)
    if np.any(np.asarray(d["z0"]).astype(np.float32)[..., W - 1] != 0): bad.append("last column of z0")
    return bad
def reference(bills, due, z0, wt):
    e = bills.astype(np.int64).reshape(N, 8, 16, L); a = due.astype(np.float32).astype(np.int64).reshape(N, 8, 16, L)
    z = z0.astype(np.float32).astype(np.int64).reshape(N, 8, 16, W); w = wt.astype(np.float32).astype(np.int64).reshape(N, 8, 16, 1)
    lower = np.tri(L, k=-1).astype(bool)
    for rnd in range(RO):
        after = []; where_to = []
        for q in range(N):
            v = np.take_along_axis(z[q], e[q].reshape(8, 1, 16 * L), 2).reshape(8, 16, 16, L)
            covers = np.add.reduce((v >= a[q][:, :, None, :]).astype(np.int64), axis=1)
            k = np.max(np.where(covers >= H, ROW, -1), axis=1)
            has = k >= 0; x = np.take_along_axis(e[q], np.maximum(k, 0)[:, None, :], 1)[:, 0]
            x = np.where(has, x, W - 1)
            wait = has & np.any((x[:, :, None] == x[:, None, :]) & lower, axis=2); pays = has & ~wait
            new = np.maximum(np.take_along_axis(z[q], x[:, None, :], 2) - a[q], 0)
            for g in range(8):
                zg = z[q, g]; m = pays[g]; zg[:, x[g][m]] = new[g][:, m]
            c = np.add.reduce(w[q] * new, axis=1) & (W - 1)
            go = pays & (k > 0) & (k < 15); kk = k[:, None, :]
            longer = np.where(ROW <= kk, e[q], np.where(ROW == kk + 1, c[:, None, :], W - 1))
            after.append(np.where(go[:, None, :], longer, e[q]))
            where_to.append(np.where(wait, q, np.where(go, c & (N - 1), -1)))
        e2 = np.full((N, 8, 16, L), W - 1, np.int64); a2 = np.ones((N, 8, 16, L), np.int64)
        for q in range(N):
            for g in range(8):
                for d in range(N):
                    ln = np.flatnonzero(where_to[q][g] == d)[:C]; at = C * q; h = (g + (d != q)) % 8
                    e2[d, h][:, at:at + len(ln)] = after[q][g][:, ln]
                    a2[d, h][:, at:at + len(ln)] = a[q, g][:, ln]
        e, a = e2, a2
    return {"yz": z.reshape(N, 128, W).astype(np.float32).astype(BF), "ye": e.reshape(N, 128, L).astype(np.float32), "ya": a.reshape(N, 128, L).astype(np.float32).astype(BF)}

@@ -1,0 +1,498 @@
+from concourse.bass import DstId, RemoteDMATransfer
+from concourse.mybir import AluOpType, ActivationFunctionType
+
+ALU = AluOpType
+ACT = ActivationFunctionType
+NR, L, W, C, RO = 8, 384, 4096, 48, 3
+ZW = W + L
+WINW = 9 * L
+MAGIC = 12582912.0
+EMPTY = -2048.0 + 1.0 / 1024
+SSETS = [[9, 10], [11, 12], [13, 14, 15]]
+S0 = SSETS[0][0]
+SPLIT = 6
+
+
+def _sb(shape, dtype):
+    return ("sbuf", [128] + shape, dtype)
+
+
+SCRATCH = {
+    "z": _sb([ZW], "bfloat16"), "xt": _sb([ZW], "float32"),
+    "bi": _sb([L], "int32"), "wb": _sb([8], "bfloat16"),
+    "pidx": _sb([8], "int32"), "pint": _sb([4], "int32"), "cols": _sb([32], "float32"),
+    "tric": _sb([16], "float32"), "e16": _sb([16], "float32"),
+    "jw": _sb([176], "int32"), "jw2": _sb([176], "int32"), "cg": _sb([128], "float32"), "rc": _sb([128], "float32"),
+    "cidx": _sb([144], "float32"), "kcon": _sb([L], "bfloat16"), "sent0": _sb([24], "float32"), "sent": _sb([24], "float32"),
+    "jb": _sb([176], "bfloat16"), "njb": _sb([176], "bfloat16"), "jk": _sb([176], "bfloat16"), "nj8": _sb([176], "bfloat16"),
+    "fs0": _sb([176], "bfloat16"), "fs1": _sb([176], "bfloat16"), "j32k": _sb([176], "float32"), "j32": _sb([176], "float32"),
+    "j16": _sb([176], "float16"), "nj16k": _sb([176], "float16"), "nm0": _sb([176], "float16"), "nm1": _sb([176], "float16"),
+    "bw": _sb([144], "bfloat16"), "rw0": _sb([144], "float16"), "rw1": _sb([144], "float16"),
+    "bo": _sb([128], "bfloat16"), "ug": _sb([128], "bfloat16"), "bc": _sb([128], "bfloat16"), "tri": _sb([15 * 128], "bfloat16"),
+    "wd8": _sb([128], "bfloat16"), "w8": _sb([128], "bfloat16"), "nw": _sb([128], "bfloat16"), "ku": _sb([128], "bfloat16"),
+    "kc0": _sb([128], "bfloat16"), "kc": _sb([128], "bfloat16"), "b2k": _sb([128], "bfloat16"),
+    "sga": _sb([128], "bfloat16"), "sgb": _sb([128], "bfloat16"), "crow": _sb([256], "bfloat16"),
+    "ones": _sb([L], "bfloat16"), "keepc": _sb([L], "bfloat16"), "d0c": _sb([L], "bfloat16"),
+    "n16": _sb([L], "float16"), "nt": _sb([12, 2, 16], "float16"), "a": _sb([L], "bfloat16"),
+    "lst": _sb([L], "uint16"), "mv": _sb([16 * L], "bfloat16"), "v": _sb([(16 - S0) * L], "bfloat16"),
+    "s": _sb([L], "bfloat16"), "st": _sb([12, 2, 16], "bfloat16"), "kp": _sb([L], "bfloat16"),
+    "f": _sb([L], "float32"), "r": _sb([L], "float32"), "xa": _sb([24], "int32"), "xi": _sb([24], "int32"),
+    "xl": _sb([24], "uint16"), "wf": _sb([24], "float32"), "x16": _sb([L], "float16"), "zx": _sb([L], "bfloat16"),
+    "new": _sb([L], "bfloat16"), "eq": _sb([24, L], "bfloat16"), "t1": _sb([L], "float32"), "ru": _sb([L], "float32"),
+    "qs": _sb([L], "bfloat16"), "oh": _sb([L], "bfloat16"), "y": _sb([12, 2, 16], "float16"), "m": _sb([L], "bfloat16"),
+    "r2": _sb([L], "float32"), "q0": _sb([L], "float32"), "sl": _sb([12, 32], "float32"), "sll": _sb([24], "uint16"),
+    "zp": _sb([24], "float32"), "zd": _sb([24], "float32"), "ze": _sb([24], "float32"), "zf": _sb([24], "float32"),
+    "zl": _sb([24], "uint16"), "oe": _sb([L], "float32"), "oa": _sb([L], "bfloat16"),
+}
+for _k in range(RO):
+    SCRATCH["win%d" % _k] = _sb([WINW], "float32")
+    SCRATCH["arr%d" % _k] = _sb([L], "float32")
+for _k in (0, 2, 3, 4, 5, 7):
+    SCRATCH["P%d" % _k] = ("psum", [128, 512], "float32")
+for _k in (1, 6):
+    SCRATCH["P%d" % _k] = ("psum", [128, 16, 2, 16], "float32")
+
+SEMAPHORES = ["cV", "cS", "cT", "cG", "sent", "arr0", "arr1", "arr2"] + ["dma%d" % _k for _k in range(12)]
+
+
+def send_calls(topo, cores, src):
+    here = topo.chip(src)
+    near = [c for c in cores if c != src and topo.chip(c) == here]
+    far = sorted((c for c in cores if topo.chip(c) != here), key=lambda c: topo.mates(topo.chip(c), here))
+    pool = topo.engines(src, far[0])
+    calls = []
+    for part in (far[:4], far[4:]):
+        n = len(pool) // len(part)
+        calls.append({c: pool[n * k:n * k + n] for k, c in enumerate(part)})
+    for c in near:
+        calls[0][c] = [e for e in topo.engines(src, c) if e not in pool]
+    return calls
+
+
+def rank_program(g, core, T, topo):
+    q = T.rank_of(core)
+    if q is None:
+        return
+    cores = list(T.cores)
+    queue = {"V": g.vector, "S": g.scalar, "T": g.tensor, "G": g, "Y": g.sync}
+    ops = []
+    ndma = [0]
+
+    def op(eng, fn, rd, wr, sem=None, val=None):
+        ops.append({"q": eng, "fn": fn, "rd": rd.split(), "wr": wr.split(), "sem": sem, "val": val})
+
+    def dma(eng, out, in_, rd, wr):
+        op(eng, lambda: queue[eng].dma_start(out, in_), rd, wr, "dma%d" % ndma[0], 16)
+        ndma[0] += 1
+
+    def ts(out, in0, s1, s2, o0, o1, rd, wr):
+        if o1 is None:
+            op("V", lambda: g.vector.tensor_scalar(out, in0, s1, None, o0), rd, wr)
+        else:
+            op("V", lambda: g.vector.tensor_scalar(out, in0, s1, s2, o0, o1), rd, wr)
+
+    def tt(out, in0, in1, o, rd, wr):
+        op("V", lambda: g.vector.tensor_tensor(out, in0, in1, o), rd, wr)
+
+    def cp(out, in_, rd, wr):
+        op("V", lambda: g.vector.tensor_copy(out, in_), rd, wr)
+
+    def ms(out, c, wr):
+        op("V", lambda: g.vector.memset(out, c), "", wr)
+
+    def tr(out, in_, rd, wr):
+        op("V", lambda: g.vector.transpose(out, in_), rd, wr)
+
+    def scan(out, d0, d1, init, o0, o1, rd, wr):
+        op("V", lambda: g.vector.tensor_tensor_scan(out, d0, d1, init, o0, o1), rd, wr)
+
+    def act(out, in_, func, bias, scale, rd, wr):
+        op("S", lambda: g.scalar.activation(out, in_, func, bias=bias, scale=scale), rd, wr)
+
+    def mm(out, lhsT, rhs, start, stop, rd, wr):
+        op("T", lambda: g.tensor.matmul(out, lhsT, rhs, start, stop), rd, wr)
+
+    def iota(out, pattern, base, cm, wr, flag=True):
+        if flag:
+            op("G", lambda: g.iota(out, pattern, base, cm, allow_small_or_imprecise_dtypes=True), "", wr)
+        else:
+            op("G", lambda: g.iota(out, pattern, base, cm), "", wr)
+
+    def col(k):
+        return T.cols[:, k:k + 1]
+
+    def row_is(k):
+        return T.e16[:, k:k + 1]
+
+    def row_lt(k):
+        return T.tric[:, k:k + 1]
+
+    def J(buf, d):
+        return buf[:, 32 - d:160 - d]
+
+    ID, RELU, SIGN = ACT.Identity, ACT.Relu, ACT.Sign
+    MUL, ADD, SUB, EQ = ALU.mult, ALU.add, ALU.subtract, ALU.is_equal
+    P0, P2, P3, P4, P5, P7 = (T["P%d" % k][:, 0:L] for k in (0, 2, 3, 4, 5, 7))
+    P1, P6 = (T["P%d" % k][:, 0:12] for k in (1, 6))
+    A = T.a[:]
+
+    dma("Y", T.bi[:], T.bills[:], "", "bi")
+    dma("S", A, T.due[:], "", "a0")
+    dma("Y", T.z[:, 0:W // 2], T.z0[:, 0:W // 2], "", "z")
+    dma("S", T.z[:, W // 2:W], T.z0[:, W // 2:W], "", "zB")
+    dma("Y", T.wb[:, 0:1], T.wt[:], "", "wb")
+
+    def prefill(k):
+        for d in range(NR):
+            ms(T["win%d" % k][:, L * d:L * d + C], EMPTY, "win%d_%d" % (k, d))
+
+    def tri(j, eng):
+        out = T.tri[:, (j - 1) * 128:j * 128]
+        if eng == "V":
+            ts(out, T.bc[:], row_lt(j), None, MUL, None, "bc tric", "tri%d" % j)
+        else:
+            act(out, T.bc[:], ID, 0.0, row_lt(j), "bc tric", "tri%d" % j)
+
+    iota(T.pidx[:, 0:1], [[0, 1]], 0, 1, "pidx", False)
+    iota(T.jw[:], [[1, 176]], 256 - 32, -1, "jw", False)
+    iota(T.cg[:], [[16, 8], [0, 16]], 0, 0, "cg")
+    iota(T.rc[:], [[0, 8], [1, 16]], 0, 0, "rc")
+    iota(T.cidx[:], [[1, 144]], -1, 0, "cidx")
+    iota(T.kcon[0:1, :], [[0, 24], [8192, 16]], (5 - 128) * 2048, 0, "kcon")
+    iota(T.sent0[:], [[16, 24]], W + 1, 0, "sent0")
+    ms(T.ones[:], 1.0, "ones")
+    for k, b in enumerate((15, 112, 16, 96)):
+        ts(T.pint[:, k:k + 1], T.pidx[:, 0:1], b, None, ALU.bitwise_and, None, "pidx", "pint%d" % k)
+    ms(T.z[:, W:ZW], 0.0, "zC")
+    cp(T.cols[:, 0:4], T.pint[:], "pint0 pint1 pint2 pint3", "c0")
+    ts(T.jw2[:], T.jw[:], 127, None, ALU.bitwise_and, None, "jw", "jw2")
+    ts(col(4), col(2), 0.0, -1.0, EQ, MUL, "c0", "c4")
+    ts(col(5), col(2), 16.0, -1.0, EQ, MUL, "c0", "c5")
+    ts(T.jb[:], T.jw2[:], 0.0, None, EQ, None, "jw2", "jb")
+    ts(T.bo[:], T.cg[:], col(1), None, EQ, None, "cg c0", "bo")
+    ts(T.nm0[:], T.jw2[:], 0.0, col(4), EQ, MUL, "jw2 c4", "nm0")
+    ts(T.e16[:], T.rc[:, 0:16], col(0), None, EQ, None, "rc c0", "e16")
+    ts(T.tric[:], T.rc[:, 0:16], col(0), None, ALU.is_gt, None, "rc c0", "tric")
+    ts(T.nm1[:], T.jw2[:], 0.0, col(5), EQ, MUL, "jw2 c5", "nm1")
+    op("G", lambda: g.affine_select(T.ug[:], T.bo[:], [[-1, 128]], ALU.is_ge, 0.0, 0, 1), "bo", "ug")
+    iota(T.xt[:, 0:W], [[1, W]], -2048, 0, "xt")
+    act(col(6), col(1), ID, 14.0, 1.0, "c0", "c6")
+    act(col(7), col(4), ID, 0.0, -262144.0, "c4", "c7")
+    act(col(8), col(5), ID, 0.0, -262144.0, "c5", "c8")
+    act(col(11), col(0), ID, 15.0, -1.0, "c0", "c11")
+    act(col(26), col(0), ID, -4092.0, -4095.0, "c0", "c26")
+    act(col(27), col(0), ID, -1729.0, 384.0, "c0", "c27")
+    act(T.njb[:], T.jb[:], ID, 0.0, -1.0, "jb", "njb")
+    act(T.bc[:], T.bo[:], ID, 0.0, 1.0, "bo", "bc")
+    act(T.jk[:], T.jb[:], ID, 0.0, 1.0 / 1024, "jb", "jk")
+    act(T.bc[:, q:128:16], T.bo[:, q:128:16], ID, 0.0, -2.0, "bo", "bc")
+    act(T.nj8[:], T.jb[:], ID, 0.0, -8192.0, "jb", "nj8")
+    act(T.bc[:, 9:128:16], T.bo[:, 9:128:16], ID, 0.0, -1.0, "bo", "bc")
+    act(col(10), row_lt(S0), ID, 3.0, -9.5, "tric", "c10")
+    act(col(30), row_is(10), ID, row_lt(9), 1.0, "e16 tric", "c30")
+    act(col(29), row_is(10), ID, col(3), 2.0, "e16 c0", "c29")
+    act(col(12), col(30), ID, 0.0, col(4), "c30 c4", "c12")
+    act(col(13), col(30), ID, 0.0, col(5), "c30 c5", "c13")
+    ms(T.keepc[:], 1.0, "keepc")
+    ts(T.bw[:], T.cidx[:], col(6), None, EQ, None, "cidx c6", "bw")
+    cp(T.j16[:], T.jb[:], "jb", "j16")
+    ts(T.n16[:], T.bi[:], -1.0, 2047.0, MUL, ADD, "bi", "n16")
+    ms(T.keepc[:, 0:L:16], 0.0, "keepc")
+    tr(T.nt[:], T.n16[:], "n16", "nt")
+    ts(T.sent[:], T.sent0[:], col(0), None, ADD, None, "sent0 c0", "sent")
+    ts(col(22), row_lt(8), -MAGIC, row_is(9), MUL, SUB, "tric e16", "c22")
+    tt(col(14), row_is(1), row_is(15), SUB, "e16", "c14")
+    ts(T.wd8[:], T.bo[:], T.wb[:, 0:1], 0.125, MUL, MUL, "bo wb", "wd8")
+    ts(col(25), row_is(10), -0.5, col(22), MUL, ADD, "e16 c22", "c25")
+    ts(T.ku[:], T.bo[:], col(14), -0.5, MUL, MUL, "bo c14", "ku")
+    act(T.fs0[:], T.jb[:], ID, 0.0, col(7), "jb c7", "fs0")
+    act(T.fs1[:], T.jb[:], ID, 0.0, col(8), "jb c8", "fs1")
+    act(T.j32k[:], T.jb[:], ID, 0.0, 1024.0, "jb", "j32k")
+    act(T.j32[:], T.jb[:], ID, 0.0, 1.0, "jb", "j32")
+    act(T.b2k[:], T.bo[:], ID, 0.0, 2048.0, "bo", "b2k")
+    act(T.crow[0:1, 0:128], T.rc[0:1, :], RELU, 1.0, -0.125, "rc", "crowA")
+    act(T.crow[0:1, 128:256], T.rc[0:1, :], ID, -0.4375, -0.125, "rc", "crowB")
+    for j in range(2, 16, 2):
+        tri(j, "S")
+    act(T.w8[:], T.wd8[:], ID, 0.0, 1.0, "wd8", "w8")
+    act(T.nw[:], T.wd8[:], ID, 0.0, -8.0, "wd8", "nw")
+    for k in (8, 9, 10):
+        act(T.w8[:, k:128:16], T.bo[:, k:128:16], ID, 0.0, 0.0, "bo", "w8")
+
+    def early():
+        ts(T.ku[:, 8:128:16], T.bo[:, 8:128:16], col(14), 0.5, MUL, MUL, "bo c14", "ku")
+        ts(T.kc0[:], J(T.jb, 1), row_lt(15), 8192.0, MUL, MUL, "jb tric", "kc0")
+        ms(T.ku[:, 9:128:16], 0.0, "ku")
+        ts(T.sga[:], T.bo[:], row_is(9), -16384.0, MUL, MUL, "bo e16", "sga")
+        ts(T.ku[:, 10:128:16], T.bo[:, 10:128:16], row_is(0), -0.5, MUL, MUL, "bo e16", "ku")
+        ts(T.sgb[:], T.bo[:], row_is(9), -2.0, MUL, MUL, "bo e16", "sgb")
+        tt(T.kc[:], T.kc0[:], J(T.nj8, 0), ADD, "kc0 nj8", "kc")
+
+    def late():
+        ms(T.xt[:, W:ZW], 0.5, "xtB")
+        prefill(0)
+
+    def later():
+        for j in range(1, 16, 2):
+            tri(j, "V")
+
+    def last():
+        ts(T.d0c[:], T.ones[:], row_lt(9), None, MUL, None, "ones tric", "d0c")
+        ts(T.rw0[:], T.cidx[:], col(29), col(12), EQ, MUL, "cidx c29 c12", "rw0")
+        ts(T.rw1[:], T.cidx[:], col(29), col(13), EQ, MUL, "cidx c29 c13", "rw1")
+        ts(T.nj16k[:], T.jb[:], -1024.0, None, MUL, None, "jb", "nj16k")
+
+    calls = send_calls(topo, cores, core)
+    arrive = sum(len(x.get(core, ())) for c in cores if c != core for x in send_calls(topo, cores, c))
+    nsent = sum(len(v) for x in calls for v in x.values())
+
+    def unpack(k):
+        a = T["arr%d" % k]
+        rd = "arr%d own%d" % (k, k)
+        ts(T.n16[:], a[:], MAGIC, -MAGIC, ADD, ADD, rd, "n16")
+        mm(P0, J(T.j32k, 16), a[:], True, False, rd + " j32k", "P0")
+
+    def fix(bank, name, b0, b1, src, sh, start, stop, rd):
+        for h2 in range(2):
+            for h in range(2):
+                mm(bank(h2), J((b0, b1)[h2], 16 * (h - h2 + sh)), src[:, :, h, :],
+                   start and h == 0, stop and h == 1 and (start or h2 == 1), rd, name)
+
+    def keys(h):
+        return T.P2[:, 192 * h:192 * h + 192]
+
+    def lists(*rows):
+        for p in rows:
+            ts(T.lst[:, 24 * p:24 * p + 24], T.P1[:, 0:12, :, p], 2047.0, None, ADD, None, "P1", "lst%d" % p)
+
+    def zwin(lst):
+        return T.z[:, 0:ZW].indirect(lst)
+
+    ZK = "z zB zC"
+
+    def vgather(p):
+        tt(T.mv[:, p * L:(p + 1) * L], zwin(T.lst[:, 24 * p:24 * p + 24]), A, ALU.is_ge, ZK + " a0 lst%d" % p, "mv%d" % p)
+
+    def sgather(i):
+        a, b = SSETS[i][0], SSETS[i][-1] + 1
+        act(T.v[:, (a - S0) * L:(b - S0) * L], zwin(T.lst[:, 24 * a:24 * b]), ID, 0.0, 1.0,
+            ZK + "".join(" lst%d" % p for p in SSETS[i]), " ".join("v%d" % p for p in SSETS[i]))
+
+    subbank = (("P4", P4), ("P5", P5), ("P7", P7), ("P6", P6), ("P4", P4), ("P5", P5), ("P1", P1))
+
+    def suba(p):
+        name, bank = subbank[p - S0]
+        mm(bank, J(T.njb, 0), A, True, False, "a0 njb", name)
+
+    def subv(p):
+        name, bank = subbank[p - S0]
+        mm(bank, J(T.jb, 0), T.v[:, (p - S0) * L:(p - S0 + 1) * L], False, True, "jb v%d" % p, name)
+
+    def sign(p):
+        name, bank = subbank[p - S0]
+        act(T.mv[:, p * L:(p + 1) * L], bank, SIGN, 0.5, 1.0, name, "mv%d" % p)
+
+    def count(p):
+        mm(P3, T.bw[:, 15 - p:143 - p], T.mv[:, p * L:(p + 1) * L], p == 0, p == 15, "bw mv%d" % p, "P3")
+
+    def eq(u, a, b, last=False):
+        key = "eq%d_%d" % (u, a)
+        ts(T.eq[:, u, a:b], T.x16[:, 16 * u + a:16 * u + b], T.wf[:, u:u + 1], None, EQ, None, "x16 wf", key)
+        a = max(a, 16)
+        if b > a:
+            mm(T.P5[:, 16 * u + a:16 * u + b], T.bc[:], T.eq[:, u, a:b], False, last, "bc " + key, "P5")
+
+    for rnd in range(RO):
+        sh = 1 if rnd else 0
+        if rnd:
+            unpack(rnd - 1)
+            tr(T.nt[:], T.n16[:], "n16", "nt")
+            mm(P0, J(T.nj16k, 16), T.n16[:], False, True, "n16 nj16k", "P0")
+        fix(lambda h: T.P1[:, 0:12, h, :], "P1", T.nm0, T.nm1, T.nt, sh, True, True, "nt nm0 nm1")
+        if rnd:
+            act(A, P0, ID, 0.0, 1.0, "P0", "a0")
+        if rnd == 0:
+            lists(*range(16))
+            early()
+        lz = lists if rnd else (lambda *rows: None)
+        lz(9, 10, 0, 1)
+        sgather(0)
+        vgather(0)
+        lz(11, 12, 2)
+        sgather(1)
+        vgather(1)
+        suba(9); suba(10); suba(11); suba(12)
+        mm(P2, T.ones[0:1, 0:128], T.kcon[0:1, :], True, False, "ones kcon", "P2")
+        fix(keys, "P2", T.nm0, T.nm1, T.nt, sh, False, False, "nt nm0 nm1")
+        lz(13, 14, 15, 3)
+        count(0)
+        vgather(2)
+        subv(9); subv(10); count(1)
+        lz(4, 5, 6, 7, 8)
+        vgather(3)
+        mm(P0, J(T.j16, 16 * sh), T.n16[:], True, False, "n16 j16", "P0")
+        mm(P0, J(T.jk, 0), A, False, False, "a0 jk", "P0")
+        count(2)
+        sign(9); sign(10)
+        subv(11); subv(12); count(3)
+        sgather(2)
+        vgather(4)
+        count(9); suba(13); count(10); suba(14); count(4); suba(15)
+        vgather(5)
+        count(5)
+        vgather(6)
+        sign(11); sign(12)
+        subv(13); subv(14); subv(15); count(6); count(11)
+        vgather(7)
+        sign(13); count(12); count(7)
+        vgather(8)
+        sign(14); count(13); count(14)
+        sign(15)
+        count(8); count(15)
+        if rnd == 0:
+            late()
+        act(T.s[:], P3, SIGN, col(10), 1.0, "P3 c10", "s")
+        tr(T.st[:], T.s[:], "s", "st")
+        if rnd == 0:
+            later()
+        mm(P1, T.ug[:], T.s[:], True, True, "ug s", "P1")
+        fix(keys, "P2", T.fs0, T.fs1, T.st, 0, False, True, "st fs0 fs1")
+        act(T.kp[:], P1, SIGN, col(11), 1.0, "P1 c11", "kp")
+        act(T.f[:], A, ID, -2048.0, 1.0 / 1024, "a0", "f")
+        scan(T.r[:], T.keepc[:], P2, 0.0, MUL, ALU.max, "keepc P2", "r")
+        mm(P4, J(T.njb, 0), A, True, False, "a0 njb", "P4")
+        mm(P5, T.crow[0:1, 0:128], T.ones[0:1, :], True, False, "crowA ones", "P5")
+        mm(P3, T.crow[0:1, 128:256], T.ones[0:1, :], True, False, "crowB ones", "P3")
+        mm(P5, T.ku[:], T.kp[:], False, False, "ku kp", "P5")
+        mm(P7, J(T.njb, 0), T.kp[:], True, False, "njb kp", "P7")
+        for h in range(2):
+            tt(T.xa[:, h:24:2], T.r[:, 192 * h + 15:192 * h + 192:16], T.sent[:, h:24:2], ALU.max, "r sent", "xa%d" % h)
+        ts(T.xi[:], T.xa[:], 8191, None, ALU.bitwise_and, None, "xa0 xa1", "xi")
+        ts(T.xl[:], T.xi[:], -1.0, None, ADD, None, "xi", "xl")
+        ts(T.wf[:], T.xi[:], -2049.0, None, ADD, None, "xi", "wf")
+        mm(P2, T.kc[:], T.kp[:], True, False, "kc kp", "P2")
+        cp(T.x16[:], T.xt[:, 0:ZW].indirect(T.xl[:]), "xt xtB xl", "x16")
+        act(T.zx[:], zwin(T.xl[:]), ID, 0.0, 1.0, ZK + " xl", "zx")
+        mm(P4, J(T.jb, 0), T.zx[:], False, True, "jb zx", "P4")
+        act(T.new[:], P4, RELU, 0.0, 1.0, "P4", "new")
+
+        for u in range(24):
+            eq(u, 0, 128 if u < SPLIT else L - 16 * u)
+            if u == 7:
+                mm(P3, T.wd8[:], T.new[:], False, True, "wd8 new", "P3")
+                act(T.t1[:], P3, ID, MAGIC, 1.0, "P3", "t1")
+                act(T.ru[:], T.t1[:], ID, col(25), row_lt(8), "t1 c25 tric", "ru")
+                act(T.qs[:], P3, SIGN, col(26), 8.0, "P3 c26", "qs")
+                mm(P5, T.w8[:], T.new[:], False, False, "w8 new", "P5")
+        diag = " ".join("eq%d_0" % u for u in range(24))
+        for j in range(1, 16):
+            mm(T.P5[:, j:L:16], T.tri[:, (j - 1) * 128:j * 128], T.eq[:, :, j], False, False, diag + " tri%d" % j, "P5")
+        for u in range(SPLIT):
+            eq(u, 128, L - 16 * u, u == SPLIT - 1)
+        mm(P2, T.nw[:], T.new[:], False, False, "nw new", "P2")
+        mm(P2, T.b2k[:], T.qs[:], False, False, "b2k qs", "P2")
+        if rnd == 0:
+            last()
+        tt(T.oh[:], T.ru[:], P5, ALU.is_ge, "ru P5", "oh")
+        mm(P7, T.sgb[:], T.oh[:], False, True, "sgb oh", "P7")
+        mm(P2, T.sga[:], T.oh[:], False, True, "sga oh", "P2")
+        scan(P4, T.d0c[:], T.oh[:], col(27), MUL, ADD, "d0c oh c27", "P4")
+        act(T.m[:], P7, RELU, 0.5, 0.5, "P7", "m")
+        act(T.r2[:], P2, RELU, 20479.0, 1.0, "P2", "r2")
+        tt(T.y[:], T.oh[:], P4, MUL, "oh P4", "y")
+        mm(P0, J(T.nj8, 0), T.m[:], False, True, "nj8 m", "P0")
+        for h2 in range(2):
+            for h in range(2):
+                mm(T.P6[:, 0:12, h2, :], (T.rw0, T.rw1)[h2][:, 1 - h:129 - h], T.y[:, :, h, :], h == 0, h == 1, "rw0 rw1 y", "P6")
+        tt(T.q0[:], T.f[:], P0, ALU.max, "f P0", "q0")
+        tr(T.sl[:], P6, "P6", "sl")
+        ts(T.sll[:], T.sl[:, :, 0:2], -1.0, 1728.0, MUL, ADD, "sl", "sll")
+        win = T["win%d" % rnd]
+        wk = " ".join("win%d_%d" % (rnd, d) for d in range(NR))
+        tt(win[:, 0:WINW].indirect(T.sll[:]), T.q0[:], T.r2[:], ADD, "sll q0 r2", wk)
+
+        def send(call, k=rnd, w=win):
+            trs = []
+            for c, engines in call.items():
+                d = cores.index(c)
+                rid, pid, _ = topo.addr(c)
+                trs.append(RemoteDMATransfer(
+                    dst_ids=[DstId(rid=rid, pnc=pid)], dma_engine_mask=sum(1 << e for e in engines),
+                    remote_sem=T.sem["arr%d" % k], src=w[:, L * d:L * d + C], dst=T["arr%d" % k][:, C * q:C * q + C]))
+            g.remote_dma_fused(trs, local_sem=T.sem.sent)
+
+        for call in calls:
+            op("G", lambda c=call, f=send: f(c), wk, "", "remote", 0)
+        op("X", None, "", "arr%d" % rnd, "arr%d" % rnd, arrive)
+        mm(T.P7[:, 0:C], J(T.j32, -16), win[:, L * q:L * q + C], True, True, wk + " j32", "P7")
+        ts(T.zp[:], T.sl[:, :, 2:4], -1.0, None, MUL, None, "sl", "zp")
+        tt(T.zd[:], T.xi[:], T.sent[:], SUB, "xi sent", "zd")
+        tt(T.ze[:], T.zp[:], T.zd[:], MUL, "zp zd", "ze")
+        tt(T.zf[:], T.sent[:], T.ze[:], ADD, "ze sent", "zf")
+        ts(T.zl[:], T.zf[:], -1.0, None, ADD, None, "zf", "zl")
+        cp(zwin(T.zl[:]), T.new[:], "zl new", ZK)
+        act(T["arr%d" % rnd][:, C * q:C * q + C], T.P7[:, 0:C], ID, 0.0, 1.0, "P7", "own%d" % rnd)
+        if rnd + 1 < RO:
+            prefill(rnd + 1)
+
+    dma("Y", T.yz[:], T.z[:, 0:W], ZK, "")
+    unpack(RO - 1)
+    mm(P3, J(T.nj16k, 16), T.n16[:], True, True, "n16 nj16k", "P3")
+    mm(P0, J(T.nj16k, 16), T.n16[:], False, True, "n16 nj16k", "P0")
+    ts(T.oe[:], P3, 1.0 / 1024, 2047.0, MUL, ADD, "P3", "oe")
+    act(T.oa[:], P0, ID, 0.0, 1.0, "P0", "oa")
+    dma("Y", T.ye[:], T.oe[:], "oe", "")
+    dma("S", T.ya[:], T.oa[:], "oa", "")
+
+    lastw, readers, know, pos = {}, {}, {k: {} for k in queue}, {k: 0 for k in "VSTG"}
+    for i, o in enumerate(ops):
+        deps = set()
+        for k in o["rd"]:
+            deps.update(lastw.get(k, ()))
+            if k[0] == "P":
+                deps.update(j for j in readers.get(k, ()) if ops[j]["q"] != o["q"])
+        for k in o["wr"]:
+            deps.update(lastw.get(k, ()))
+            deps.update(readers.get(k, ()))
+        for k in o["rd"]:
+            readers.setdefault(k, []).append(i)
+        for k in o["wr"]:
+            lastw[k], readers[k] = [i], []
+        if o["sem"] is None:
+            pos[o["q"]] += 1
+            o["id"] = (o["q"], pos[o["q"]])
+        else:
+            o["id"] = (o["sem"], 1)
+        o["waits"] = []
+        kn = know.get(o["q"], {})
+        for j in sorted(deps, reverse=True):
+            d = ops[j]
+            if j == i or (d["q"] == "T" and o["q"] == "T") or kn.get(d["id"][0], 0) >= d["id"][1]:
+                continue
+            o["waits"].append(j)
+            d["mark"] = True
+            for k, v in d["clock"].items():
+                kn[k] = max(kn.get(k, 0), v)
+        o["clock"] = dict(kn)
+        o["clock"][o["id"][0]] = o["id"][1]
+    total = {k: 0 for k in "VSTG"}
+    for o in ops:
+        for j in o["waits"]:
+            d = ops[j]
+            queue[o["q"]].wait_ge(T.sem[d["sem"] or "c" + d["q"]], d["val"])
+        if o["fn"] is None:
+            continue
+        ins = o["fn"]()
+        if o["sem"] is None:
+            if o.get("mark"):
+                total[o["q"]] += 1
+                o["val"] = total[o["q"]]
+                ins.then_inc(T.sem["c" + o["q"]], 1)
+        elif o["sem"] != "remote":
+            ins.then_inc(T.sem[o["sem"]], 16)
+    for k in "VSTG":
+        if total[k]:
+            g.wait_ge(T.sem["c" + k], total[k])
+    g.wait_ge(T.sem.sent, RO * nsent)
+    for k in range(ndma[0]):
+        g.wait_ge(T.sem["dma%d" % k], 16)

@@ -4,11 +4,12 @@ from concourse.mybir import AluOpType, ActivationFunctionType
 ALU = AluOpType
 ACT = ActivationFunctionType
 NR, L, W, C, RO = 8, 384, 4096, 48, 3
-ZW = W + L
+PAD = 16
+ZW = PAD + W + L
 WINW = 9 * L
 MAGIC = 12582912.0
 EMPTY = -2048.0 + 1.0 / 1024
-SSETS = [[9, 10], [11, 12], [13, 14, 15]]
+SSETS = [[10, 11], [12, 13], [14, 15]]
 S0 = SSETS[0][0]
 SPLIT = 6
 
@@ -17,42 +18,24 @@ def _sb(shape, dtype):
     return ("sbuf", [128] + shape, dtype)
 
 
-SCRATCH = {
-    "z": _sb([ZW], "bfloat16"), "xt": _sb([ZW], "float32"),
-    "bi": _sb([L], "int32"), "wb": _sb([8], "bfloat16"),
-    "pidx": _sb([8], "int32"), "pint": _sb([4], "int32"), "cols": _sb([32], "float32"),
-    "tric": _sb([16], "float32"), "e16": _sb([16], "float32"),
-    "jw": _sb([176], "int32"), "jw2": _sb([176], "int32"), "cg": _sb([128], "float32"), "rc": _sb([128], "float32"),
-    "cidx": _sb([144], "float32"), "kcon": _sb([L], "bfloat16"), "sent0": _sb([24], "float32"), "sent": _sb([24], "float32"),
-    "jb": _sb([176], "bfloat16"), "njb": _sb([176], "bfloat16"), "jk": _sb([176], "bfloat16"), "nj8": _sb([176], "bfloat16"),
-    "fs0": _sb([176], "bfloat16"), "fs1": _sb([176], "bfloat16"), "j32k": _sb([176], "float32"), "j32": _sb([176], "float32"),
-    "j16": _sb([176], "float16"), "nj16k": _sb([176], "float16"), "nm0": _sb([176], "float16"), "nm1": _sb([176], "float16"),
-    "bw": _sb([144], "bfloat16"), "rw0": _sb([144], "float16"), "rw1": _sb([144], "float16"),
-    "bo": _sb([128], "bfloat16"), "ug": _sb([128], "bfloat16"), "bc": _sb([128], "bfloat16"), "tri": _sb([15 * 128], "bfloat16"),
-    "wd8": _sb([128], "bfloat16"), "w8": _sb([128], "bfloat16"), "nw": _sb([128], "bfloat16"), "ku": _sb([128], "bfloat16"),
-    "kc0": _sb([128], "bfloat16"), "kc": _sb([128], "bfloat16"), "b2k": _sb([128], "bfloat16"),
-    "sga": _sb([128], "bfloat16"), "sgb": _sb([128], "bfloat16"), "crow": _sb([256], "bfloat16"),
-    "ones": _sb([L], "bfloat16"), "keepc": _sb([L], "bfloat16"), "d0c": _sb([L], "bfloat16"),
-    "n16": _sb([L], "float16"), "nt": _sb([12, 2, 16], "float16"), "a": _sb([L], "bfloat16"),
-    "lst": _sb([L], "uint16"), "mv": _sb([16 * L], "bfloat16"), "v": _sb([(16 - S0) * L], "bfloat16"),
-    "s": _sb([L], "bfloat16"), "st": _sb([12, 2, 16], "bfloat16"), "kp": _sb([L], "bfloat16"),
-    "f": _sb([L], "float32"), "r": _sb([L], "float32"), "xa": _sb([24], "int32"), "xi": _sb([24], "int32"),
-    "xl": _sb([24], "uint16"), "wf": _sb([24], "float32"), "x16": _sb([L], "float16"), "zx": _sb([L], "bfloat16"),
-    "new": _sb([L], "bfloat16"), "eq": _sb([24, L], "bfloat16"), "t1": _sb([L], "float32"), "ru": _sb([L], "float32"),
-    "qs": _sb([L], "bfloat16"), "oh": _sb([L], "bfloat16"), "y": _sb([12, 2, 16], "float16"), "m": _sb([L], "bfloat16"),
-    "r2": _sb([L], "float32"), "q0": _sb([L], "float32"), "sl": _sb([12, 32], "float32"), "sll": _sb([24], "uint16"),
-    "zp": _sb([24], "float32"), "zd": _sb([24], "float32"), "ze": _sb([24], "float32"), "zf": _sb([24], "float32"),
-    "zl": _sb([24], "uint16"), "oe": _sb([L], "float32"), "oa": _sb([L], "bfloat16"),
-}
-for _k in range(RO):
-    SCRATCH["win%d" % _k] = _sb([WINW], "float32")
-    SCRATCH["arr%d" % _k] = _sb([L], "float32")
-for _k in (0, 2, 3, 4, 5, 7):
+SCRATCH = {"nt": _sb([12, 2, 16], "float16"), "eq": _sb([24, L], "bfloat16")}
+for _d, _n, _names in (
+        ("bfloat16", ZW, "z"), ("int32", L, "bi"), ("bfloat16", 8, "wb"), ("int32", 8, "pidx"),
+        ("int32", 4, "pint"), ("float32", 32, "cols"), ("float32", 16, "tric e16"), ("int32", 176, "jw jw2"),
+        ("float32", 128, "cg rc"), ("float32", 144, "cidx"), ("float32", 24, "sent0 sent wf zc zd ze zf"),
+        ("bfloat16", 176, "jb njb jk nj8"), ("float32", 176, "j32k j32"), ("float16", 176, "j16 nj16 nj16k nm0 nm1"),
+        ("bfloat16", 144, "bw bw10"), ("float16", 144, "bw16 bw9"), ("bfloat16", 15 * 128, "tri"), ("float16", 128, "bo16"),
+        ("bfloat16", 128, "bo ug ug4 vu bc wd8 nw ku kc0 kc b2k sga sgb"), ("bfloat16", 256, "crow"),
+        ("bfloat16", L, "ones a s kp zx new qs oh m oa"), ("float16", L, "n16 x16 yp y"),
+        ("float32", L, "f t1 ru r2 q0 oe arr0 arr1 arr2"), ("float32", WINW, "win0 win1 win2"),
+        ("uint16", L, "lst"), ("bfloat16", 16 * L, "mv"), ("bfloat16", (16 - S0) * L, "v"), ("uint16", 24, "xl sll zl")):
+    for _k in _names.split():
+        SCRATCH[_k] = _sb([_n], _d)
+for _k in (0, 2, 3, 4, 5, 6, 7):
     SCRATCH["P%d" % _k] = ("psum", [128, 512], "float32")
-for _k in (1, 6):
-    SCRATCH["P%d" % _k] = ("psum", [128, 16, 2, 16], "float32")
+SCRATCH["P1"] = ("psum", [128, 16, 2, 16], "float32")
 
-SEMAPHORES = ["cV", "cS", "cT", "cG", "sent", "arr0", "arr1", "arr2"] + ["dma%d" % _k for _k in range(12)]
+SEMAPHORES = ["cV", "cS", "cT", "cG", "sent"] + ["arr%d" % _k for _k in range(RO)] + ["dma%d" % _k for _k in range(8)]
 
 
 def send_calls(topo, cores, src):
@@ -130,16 +113,19 @@ def rank_program(g, core, T, topo):
     def J(buf, d):
         return buf[:, 32 - d:160 - d]
 
+    def B(buf, p):
+        return buf[:, 15 - p:143 - p]
+
     ID, RELU, SIGN = ACT.Identity, ACT.Relu, ACT.Sign
     MUL, ADD, SUB, EQ = ALU.mult, ALU.add, ALU.subtract, ALU.is_equal
-    P0, P2, P3, P4, P5, P7 = (T["P%d" % k][:, 0:L] for k in (0, 2, 3, 4, 5, 7))
-    P1, P6 = (T["P%d" % k][:, 0:12] for k in (1, 6))
+    P0, P2, P3, P4, P5, P6, P7 = (T["P%d" % k][:, 0:L] for k in (0, 2, 3, 4, 5, 6, 7))
+    P1 = T.P1[:, 0:12]
     A = T.a[:]
 
     dma("Y", T.bi[:], T.bills[:], "", "bi")
     dma("S", A, T.due[:], "", "a0")
-    dma("Y", T.z[:, 0:W // 2], T.z0[:, 0:W // 2], "", "z")
-    dma("S", T.z[:, W // 2:W], T.z0[:, W // 2:W], "", "zB")
+    dma("Y", T.z[:, PAD:PAD + W // 2], T.z0[:, 0:W // 2], "", "z")
+    dma("S", T.z[:, PAD + W // 2:PAD + W], T.z0[:, W // 2:W], "", "zB")
     dma("Y", T.wb[:, 0:1], T.wt[:], "", "wb")
 
     def prefill(k):
@@ -158,13 +144,13 @@ def rank_program(g, core, T, topo):
     iota(T.cg[:], [[16, 8], [0, 16]], 0, 0, "cg")
     iota(T.rc[:], [[0, 8], [1, 16]], 0, 0, "rc")
     iota(T.cidx[:], [[1, 144]], -1, 0, "cidx")
-    iota(T.kcon[0:1, :], [[0, 24], [8192, 16]], (5 - 128) * 2048, 0, "kcon")
-    iota(T.sent0[:], [[16, 24]], W + 1, 0, "sent0")
+    iota(T.sent0[:], [[16, 24]], PAD + W, 0, "sent0")
     ms(T.ones[:], 1.0, "ones")
-    for k, b in enumerate((15, 112, 16, 96)):
+    for k, b in enumerate((15, 112, 16)):
         ts(T.pint[:, k:k + 1], T.pidx[:, 0:1], b, None, ALU.bitwise_and, None, "pidx", "pint%d" % k)
-    ms(T.z[:, W:ZW], 0.0, "zC")
-    cp(T.cols[:, 0:4], T.pint[:], "pint0 pint1 pint2 pint3", "c0")
+    ms(T.z[:, PAD + W:ZW], 0.0, "zC")
+    ms(T.z[:, 0:PAD], 0.0, "zD")
+    cp(T.cols[:, 0:3], T.pint[:, 0:3], "pint0 pint1 pint2", "c0")
     ts(T.jw2[:], T.jw[:], 127, None, ALU.bitwise_and, None, "jw", "jw2")
     ts(col(4), col(2), 0.0, -1.0, EQ, MUL, "c0", "c4")
     ts(col(5), col(2), 16.0, -1.0, EQ, MUL, "c0", "c5")
@@ -175,10 +161,8 @@ def rank_program(g, core, T, topo):
     ts(T.tric[:], T.rc[:, 0:16], col(0), None, ALU.is_gt, None, "rc c0", "tric")
     ts(T.nm1[:], T.jw2[:], 0.0, col(5), EQ, MUL, "jw2 c5", "nm1")
     op("G", lambda: g.affine_select(T.ug[:], T.bo[:], [[-1, 128]], ALU.is_ge, 0.0, 0, 1), "bo", "ug")
-    iota(T.xt[:, 0:W], [[1, W]], -2048, 0, "xt")
     act(col(6), col(1), ID, 14.0, 1.0, "c0", "c6")
-    act(col(7), col(4), ID, 0.0, -262144.0, "c4", "c7")
-    act(col(8), col(5), ID, 0.0, -262144.0, "c5", "c8")
+    act(col(7), col(0), ID, -65536.0, 4096.0, "c0", "c7")
     act(col(11), col(0), ID, 15.0, -1.0, "c0", "c11")
     act(col(26), col(0), ID, -4092.0, -4095.0, "c0", "c26")
     act(col(27), col(0), ID, -1729.0, 384.0, "c0", "c27")
@@ -189,57 +173,45 @@ def rank_program(g, core, T, topo):
     act(T.nj8[:], T.jb[:], ID, 0.0, -8192.0, "jb", "nj8")
     act(T.bc[:, 9:128:16], T.bo[:, 9:128:16], ID, 0.0, -1.0, "bo", "bc")
     act(col(10), row_lt(S0), ID, 3.0, -9.5, "tric", "c10")
-    act(col(30), row_is(10), ID, row_lt(9), 1.0, "e16 tric", "c30")
-    act(col(29), row_is(10), ID, col(3), 2.0, "e16 c0", "c29")
-    act(col(12), col(30), ID, 0.0, col(4), "c30 c4", "c12")
-    act(col(13), col(30), ID, 0.0, col(5), "c30 c5", "c13")
-    ms(T.keepc[:], 1.0, "keepc")
+    act(T.crow[0:1, 0:128], T.rc[0:1, :], ID, 1.4375, 0.0, "rc", "crowA")
     ts(T.bw[:], T.cidx[:], col(6), None, EQ, None, "cidx c6", "bw")
     cp(T.j16[:], T.jb[:], "jb", "j16")
+    ts(T.nj16[:], T.jb[:], -1.0, None, MUL, None, "jb", "nj16")
+    cp(T.bo16[:], T.bo[:], "bo", "bo16")
     ts(T.n16[:], T.bi[:], -1.0, 2047.0, MUL, ADD, "bi", "n16")
-    ms(T.keepc[:, 0:L:16], 0.0, "keepc")
+    cp(T.bw16[:], T.bw[:], "bw", "bw16")
     tr(T.nt[:], T.n16[:], "n16", "nt")
     ts(T.sent[:], T.sent0[:], col(0), None, ADD, None, "sent0 c0", "sent")
-    ts(col(22), row_lt(8), -MAGIC, row_is(9), MUL, SUB, "tric e16", "c22")
     tt(col(14), row_is(1), row_is(15), SUB, "e16", "c14")
     ts(T.wd8[:], T.bo[:], T.wb[:, 0:1], 0.125, MUL, MUL, "bo wb", "wd8")
-    ts(col(25), row_is(10), -0.5, col(22), MUL, ADD, "e16 c22", "c25")
+    ms(T.crow[0:1, 8:128:16], -0.4375, "crowA")
     ts(T.ku[:], T.bo[:], col(14), -0.5, MUL, MUL, "bo c14", "ku")
-    act(T.fs0[:], T.jb[:], ID, 0.0, col(7), "jb c7", "fs0")
-    act(T.fs1[:], T.jb[:], ID, 0.0, col(8), "jb c8", "fs1")
+    ms(T.crow[0:1, 9:128:16], 0.5625, "crowA")
+    act(T.ug4[:], T.ug[:], ID, 0.0, -4096.0, "ug", "ug4")
     act(T.j32k[:], T.jb[:], ID, 0.0, 1024.0, "jb", "j32k")
     act(T.j32[:], T.jb[:], ID, 0.0, 1.0, "jb", "j32")
     act(T.b2k[:], T.bo[:], ID, 0.0, 2048.0, "bo", "b2k")
-    act(T.crow[0:1, 0:128], T.rc[0:1, :], RELU, 1.0, -0.125, "rc", "crowA")
     act(T.crow[0:1, 128:256], T.rc[0:1, :], ID, -0.4375, -0.125, "rc", "crowB")
+    act(T.bw10[:], T.bw[:], ID, 0.0, row_is(10), "bw e16", "bw10")
     for j in range(2, 16, 2):
         tri(j, "S")
-    act(T.w8[:], T.wd8[:], ID, 0.0, 1.0, "wd8", "w8")
     act(T.nw[:], T.wd8[:], ID, 0.0, -8.0, "wd8", "nw")
-    for k in (8, 9, 10):
-        act(T.w8[:, k:128:16], T.bo[:, k:128:16], ID, 0.0, 0.0, "bo", "w8")
 
-    def early():
+    def late():
+        tt(T.vu[:], T.ug4[:], J(T.nj8, 0), SUB, "ug4 nj8", "vu")
+        ms(T.crow[0:1, 10:128:16], 0.0625, "crowA")
         ts(T.ku[:, 8:128:16], T.bo[:, 8:128:16], col(14), 0.5, MUL, MUL, "bo c14", "ku")
         ts(T.kc0[:], J(T.jb, 1), row_lt(15), 8192.0, MUL, MUL, "jb tric", "kc0")
         ms(T.ku[:, 9:128:16], 0.0, "ku")
         ts(T.sga[:], T.bo[:], row_is(9), -16384.0, MUL, MUL, "bo e16", "sga")
         ts(T.ku[:, 10:128:16], T.bo[:, 10:128:16], row_is(0), -0.5, MUL, MUL, "bo e16", "ku")
         ts(T.sgb[:], T.bo[:], row_is(9), -2.0, MUL, MUL, "bo e16", "sgb")
-        tt(T.kc[:], T.kc0[:], J(T.nj8, 0), ADD, "kc0 nj8", "kc")
-
-    def late():
-        ms(T.xt[:, W:ZW], 0.5, "xtB")
-        prefill(0)
-
-    def later():
         for j in range(1, 16, 2):
             tri(j, "V")
 
-    def last():
-        ts(T.d0c[:], T.ones[:], row_lt(9), None, MUL, None, "ones tric", "d0c")
-        ts(T.rw0[:], T.cidx[:], col(29), col(12), EQ, MUL, "cidx c29 c12", "rw0")
-        ts(T.rw1[:], T.cidx[:], col(29), col(13), EQ, MUL, "cidx c29 c13", "rw1")
+    def later():
+        tt(T.kc[:], T.kc0[:], J(T.nj8, 0), ADD, "kc0 nj8", "kc")
+        ts(T.bw9[:], T.bw[:], row_lt(9), None, MUL, None, "bw tric", "bw9")
         ts(T.nj16k[:], T.jb[:], -1024.0, None, MUL, None, "jb", "nj16k")
 
     calls = send_calls(topo, cores, core)
@@ -252,23 +224,18 @@ def rank_program(g, core, T, topo):
         ts(T.n16[:], a[:], MAGIC, -MAGIC, ADD, ADD, rd, "n16")
         mm(P0, J(T.j32k, 16), a[:], True, False, rd + " j32k", "P0")
 
-    def fix(bank, name, b0, b1, src, sh, start, stop, rd):
-        for h2 in range(2):
-            for h in range(2):
-                mm(bank(h2), J((b0, b1)[h2], 16 * (h - h2 + sh)), src[:, :, h, :],
-                   start and h == 0, stop and h == 1 and (start or h2 == 1), rd, name)
-
-    def keys(h):
-        return T.P2[:, 192 * h:192 * h + 192]
-
     def lists(*rows):
         for p in rows:
-            ts(T.lst[:, 24 * p:24 * p + 24], T.P1[:, 0:12, :, p], 2047.0, None, ADD, None, "P1", "lst%d" % p)
+            ts(T.lst[:, 24 * p:24 * p + 24], T.P1[:, 0:12, :, p], 2047.0 + PAD, None, ADD, None, "P1", "lst%d" % p)
+
+    def wrap(bank, name, lhs, src, rd):
+        for s in range(16):
+            mm(bank[:, 0:24], B(lhs, s), src[:, s:L:16], s == 0, s == 15, rd, name)
 
     def zwin(lst):
         return T.z[:, 0:ZW].indirect(lst)
 
-    ZK = "z zB zC"
+    ZK = "z zB zC zD"
 
     def vgather(p):
         tt(T.mv[:, p * L:(p + 1) * L], zwin(T.lst[:, 24 * p:24 * p + 24]), A, ALU.is_ge, ZK + " a0 lst%d" % p, "mv%d" % p)
@@ -278,7 +245,7 @@ def rank_program(g, core, T, topo):
         act(T.v[:, (a - S0) * L:(b - S0) * L], zwin(T.lst[:, 24 * a:24 * b]), ID, 0.0, 1.0,
             ZK + "".join(" lst%d" % p for p in SSETS[i]), " ".join("v%d" % p for p in SSETS[i]))
 
-    subbank = (("P4", P4), ("P5", P5), ("P7", P7), ("P6", P6), ("P4", P4), ("P5", P5), ("P1", P1))
+    subbank = (("P7", P7), ("P6", P6), ("P4", P4), ("P5", P5), ("P7", P7), ("P6", P6))
 
     def suba(p):
         name, bank = subbank[p - S0]
@@ -293,7 +260,7 @@ def rank_program(g, core, T, topo):
         act(T.mv[:, p * L:(p + 1) * L], bank, SIGN, 0.5, 1.0, name, "mv%d" % p)
 
     def count(p):
-        mm(P3, T.bw[:, 15 - p:143 - p], T.mv[:, p * L:(p + 1) * L], p == 0, p == 15, "bw mv%d" % p, "P3")
+        mm(P3, B(T.bw, p), T.mv[:, p * L:(p + 1) * L], p == 0, p == S0 - 1, "bw mv%d" % p, "P3")
 
     def eq(u, a, b, last=False):
         key = "eq%d_%d" % (u, a)
@@ -308,105 +275,112 @@ def rank_program(g, core, T, topo):
             unpack(rnd - 1)
             tr(T.nt[:], T.n16[:], "n16", "nt")
             mm(P0, J(T.nj16k, 16), T.n16[:], False, True, "n16 nj16k", "P0")
-        fix(lambda h: T.P1[:, 0:12, h, :], "P1", T.nm0, T.nm1, T.nt, sh, True, True, "nt nm0 nm1")
+        for h2 in range(2):
+            for h in range(2):
+                mm(T.P1[:, 0:12, h2, :], J((T.nm0, T.nm1)[h2], 16 * (h - h2 + sh)), T.nt[:, :, h, :],
+                   h == 0, h == 1, "nt nm0 nm1", "P1")
         if rnd:
             act(A, P0, ID, 0.0, 1.0, "P0", "a0")
+        lists(0, 10, 11, 1)
         if rnd == 0:
-            lists(*range(16))
-            early()
+            lists(12, 13, 2, 14, 15, 3, 4, 5, 6, 7, 8, 9)
         lz = lists if rnd else (lambda *rows: None)
-        lz(9, 10, 0, 1)
         sgather(0)
         vgather(0)
-        lz(11, 12, 2)
+        suba(10); suba(11)
+        lz(12, 13, 2)
         sgather(1)
         vgather(1)
-        suba(9); suba(10); suba(11); suba(12)
-        mm(P2, T.ones[0:1, 0:128], T.kcon[0:1, :], True, False, "ones kcon", "P2")
-        fix(keys, "P2", T.nm0, T.nm1, T.nt, sh, False, False, "nt nm0 nm1")
-        lz(13, 14, 15, 3)
+        mm(P2, J(T.nj16, 16 * sh), T.n16[:], True, False, "n16 nj16", "P2")
+        suba(12); suba(13)
+        lz(14, 15, 3)
         count(0)
         vgather(2)
-        subv(9); subv(10); count(1)
-        lz(4, 5, 6, 7, 8)
+        subv(10); subv(11); count(1)
+        lz(4, 5, 6, 7, 8, 9)
         vgather(3)
+        count(2)
         mm(P0, J(T.j16, 16 * sh), T.n16[:], True, False, "n16 j16", "P0")
         mm(P0, J(T.jk, 0), A, False, False, "a0 jk", "P0")
-        count(2)
-        sign(9); sign(10)
-        subv(11); subv(12); count(3)
+        sign(10); sign(11)
+        subv(12); subv(13); count(3)
         sgather(2)
         vgather(4)
-        count(9); suba(13); count(10); suba(14); count(4); suba(15)
+        count(10); suba(14); count(11); suba(15); count(4)
         vgather(5)
         count(5)
         vgather(6)
-        sign(11); sign(12)
-        subv(13); subv(14); subv(15); count(6); count(11)
+        sign(12); sign(13)
+        subv(14); subv(15); count(6)
         vgather(7)
-        sign(13); count(12); count(7)
+        count(12); count(13); count(7)
+        sign(14); sign(15)
         vgather(8)
-        sign(14); count(13); count(14)
-        sign(15)
-        count(8); count(15)
+        count(14); count(8)
+        vgather(9)
+        count(15); count(9)
         if rnd == 0:
             late()
+        else:
+            prefill(rnd)
         act(T.s[:], P3, SIGN, col(10), 1.0, "P3 c10", "s")
-        tr(T.st[:], T.s[:], "s", "st")
-        if rnd == 0:
-            later()
+        mm(P2, T.vu[:], T.s[:], False, True, "vu s", "P2")
         mm(P1, T.ug[:], T.s[:], True, True, "ug s", "P1")
-        fix(keys, "P2", T.fs0, T.fs1, T.st, 0, False, True, "st fs0 fs1")
-        act(T.kp[:], P1, SIGN, col(11), 1.0, "P1 c11", "kp")
-        act(T.f[:], A, ID, -2048.0, 1.0 / 1024, "a0", "f")
-        scan(T.r[:], T.keepc[:], P2, 0.0, MUL, ALU.max, "keepc P2", "r")
         mm(P4, J(T.njb, 0), A, True, False, "a0 njb", "P4")
         mm(P5, T.crow[0:1, 0:128], T.ones[0:1, :], True, False, "crowA ones", "P5")
+        ts(T.yp[:], P2, col(7), -2048.0, ADD, ALU.max, "P2 c7", "yp")
+        act(T.kp[:], P1, SIGN, col(11), 1.0, "P1 c11", "kp")
+        act(T.f[:], A, ID, -2048.0, 1.0 / 1024, "a0", "f")
+        if rnd == 0:
+            later()
+        mm(P6, T.bo16[:], T.yp[:], True, True, "bo16 yp", "P6")
+        wrap(T.P2, "P2", T.bw16, T.yp, "bw16 yp")
+        ts(T.x16[:], P6, 30720.0, None, ADD, None, "P6", "x16")
         mm(P3, T.crow[0:1, 128:256], T.ones[0:1, :], True, False, "crowB ones", "P3")
         mm(P5, T.ku[:], T.kp[:], False, False, "ku kp", "P5")
-        mm(P7, J(T.njb, 0), T.kp[:], True, False, "njb kp", "P7")
-        for h in range(2):
-            tt(T.xa[:, h:24:2], T.r[:, 192 * h + 15:192 * h + 192:16], T.sent[:, h:24:2], ALU.max, "r sent", "xa%d" % h)
-        ts(T.xi[:], T.xa[:], 8191, None, ALU.bitwise_and, None, "xa0 xa1", "xi")
-        ts(T.xl[:], T.xi[:], -1.0, None, ADD, None, "xi", "xl")
-        ts(T.wf[:], T.xi[:], -2049.0, None, ADD, None, "xi", "wf")
-        mm(P2, T.kc[:], T.kp[:], True, False, "kc kp", "P2")
-        cp(T.x16[:], T.xt[:, 0:ZW].indirect(T.xl[:]), "xt xtB xl", "x16")
+        ts(T.wf[:], T.P2[:, 0:24], 30720.0, -2047.5, ADD, ALU.max, "P2", "wf")
+        ts(T.xl[:], T.P2[:, 0:24], 32767.0 + PAD, None, ADD, None, "P2", "xl")
         act(T.zx[:], zwin(T.xl[:]), ID, 0.0, 1.0, ZK + " xl", "zx")
-        mm(P4, J(T.jb, 0), T.zx[:], False, True, "jb zx", "P4")
-        act(T.new[:], P4, RELU, 0.0, 1.0, "P4", "new")
 
-        for u in range(24):
+        order = list(range(SPLIT, 12)) + list(range(SPLIT)) + list(range(12, 24))
+        for i, u in enumerate(order):
             eq(u, 0, 128 if u < SPLIT else L - 16 * u)
-            if u == 7:
+            if i == 4:
+                mm(P4, J(T.jb, 0), T.zx[:], False, True, "jb zx", "P4")
+                act(T.new[:], P4, RELU, 0.0, 1.0, "P4", "new")
+            if i == 19:
                 mm(P3, T.wd8[:], T.new[:], False, True, "wd8 new", "P3")
-                act(T.t1[:], P3, ID, MAGIC, 1.0, "P3", "t1")
-                act(T.ru[:], T.t1[:], ID, col(25), row_lt(8), "t1 c25 tric", "ru")
-                act(T.qs[:], P3, SIGN, col(26), 8.0, "P3 c26", "qs")
-                mm(P5, T.w8[:], T.new[:], False, False, "w8 new", "P5")
         diag = " ".join("eq%d_0" % u for u in range(24))
         for j in range(1, 16):
             mm(T.P5[:, j:L:16], T.tri[:, (j - 1) * 128:j * 128], T.eq[:, :, j], False, False, diag + " tri%d" % j, "P5")
         for u in range(SPLIT):
             eq(u, 128, L - 16 * u, u == SPLIT - 1)
+        ts(T.t1[:], P3, MAGIC, -MAGIC, ADD, ADD, "P3", "t1")
+        tt(T.zc[:], T.wf[:], T.sent[:], SUB, "wf sent", "zc")
+        tt(T.ru[:], T.t1[:], P3, SUB, "t1 P3", "ru")
+        act(T.qs[:], P3, SIGN, col(26), 8.0, "P3 c26", "qs")
+        mm(P7, J(T.njb, 0), T.kp[:], True, False, "njb kp", "P7")
+        mm(P2, T.kc[:], T.kp[:], True, False, "kc kp", "P2")
         mm(P2, T.nw[:], T.new[:], False, False, "nw new", "P2")
-        mm(P2, T.b2k[:], T.qs[:], False, False, "b2k qs", "P2")
-        if rnd == 0:
-            last()
         tt(T.oh[:], T.ru[:], P5, ALU.is_ge, "ru P5", "oh")
         mm(P7, T.sgb[:], T.oh[:], False, True, "sgb oh", "P7")
+        mm(P2, T.b2k[:], T.qs[:], False, False, "b2k qs", "P2")
         mm(P2, T.sga[:], T.oh[:], False, True, "sga oh", "P2")
-        scan(P4, T.d0c[:], T.oh[:], col(27), MUL, ADD, "d0c oh c27", "P4")
+        wrap(T.P3, "P3", T.bw10, T.oh, "bw10 oh")
+        ts(T.zd[:], T.zc[:], 2047.0 + PAD, None, ADD, None, "zc", "zd")
+        scan(P4, T.ones[:], T.oh[:], col(27), MUL, ADD, "ones oh c27", "P4")
         act(T.m[:], P7, RELU, 0.5, 0.5, "P7", "m")
         act(T.r2[:], P2, RELU, 20479.0, 1.0, "P2", "r2")
         tt(T.y[:], T.oh[:], P4, MUL, "oh P4", "y")
         mm(P0, J(T.nj8, 0), T.m[:], False, True, "nj8 m", "P0")
-        for h2 in range(2):
-            for h in range(2):
-                mm(T.P6[:, 0:12, h2, :], (T.rw0, T.rw1)[h2][:, 1 - h:129 - h], T.y[:, :, h, :], h == 0, h == 1, "rw0 rw1 y", "P6")
+        wrap(T.P6, "P6", T.bw9, T.y, "bw9 y")
+        if rnd == 0:
+            prefill(0)
+        tt(T.ze[:], T.zd[:], T.P3[:, 0:24], MUL, "zd P3", "ze")
         tt(T.q0[:], T.f[:], P0, ALU.max, "f P0", "q0")
-        tr(T.sl[:], P6, "P6", "sl")
-        ts(T.sll[:], T.sl[:, :, 0:2], -1.0, 1728.0, MUL, ADD, "sl", "sll")
+        tt(T.zf[:], T.sent[:], T.ze[:], ADD, "ze sent", "zf")
+        ts(T.sll[:], T.P6[:, 0:24], 1728.0, None, ADD, None, "P6", "sll")
+        cp(T.zl[:], T.zf[:], "zf", "zl")
         win = T["win%d" % rnd]
         wk = " ".join("win%d_%d" % (rnd, d) for d in range(NR))
         tt(win[:, 0:WINW].indirect(T.sll[:]), T.q0[:], T.r2[:], ADD, "sll q0 r2", wk)
@@ -425,24 +399,17 @@ def rank_program(g, core, T, topo):
             op("G", lambda c=call, f=send: f(c), wk, "", "remote", 0)
         op("X", None, "", "arr%d" % rnd, "arr%d" % rnd, arrive)
         mm(T.P7[:, 0:C], J(T.j32, -16), win[:, L * q:L * q + C], True, True, wk + " j32", "P7")
-        ts(T.zp[:], T.sl[:, :, 2:4], -1.0, None, MUL, None, "sl", "zp")
-        tt(T.zd[:], T.xi[:], T.sent[:], SUB, "xi sent", "zd")
-        tt(T.ze[:], T.zp[:], T.zd[:], MUL, "zp zd", "ze")
-        tt(T.zf[:], T.sent[:], T.ze[:], ADD, "ze sent", "zf")
-        ts(T.zl[:], T.zf[:], -1.0, None, ADD, None, "zf", "zl")
         cp(zwin(T.zl[:]), T.new[:], "zl new", ZK)
         act(T["arr%d" % rnd][:, C * q:C * q + C], T.P7[:, 0:C], ID, 0.0, 1.0, "P7", "own%d" % rnd)
-        if rnd + 1 < RO:
-            prefill(rnd + 1)
 
-    dma("Y", T.yz[:], T.z[:, 0:W], ZK, "")
+    dma("Y", T.yz[:], T.z[:, PAD:PAD + W], ZK, "")
     unpack(RO - 1)
-    mm(P3, J(T.nj16k, 16), T.n16[:], True, True, "n16 nj16k", "P3")
     mm(P0, J(T.nj16k, 16), T.n16[:], False, True, "n16 nj16k", "P0")
-    ts(T.oe[:], P3, 1.0 / 1024, 2047.0, MUL, ADD, "P3", "oe")
+    mm(P3, J(T.nj16k, 16), T.n16[:], True, True, "n16 nj16k", "P3")
     act(T.oa[:], P0, ID, 0.0, 1.0, "P0", "oa")
-    dma("Y", T.ye[:], T.oe[:], "oe", "")
+    ts(T.oe[:], P3, 1.0 / 1024, 2047.0, MUL, ADD, "P3", "oe")
     dma("S", T.ya[:], T.oa[:], "oa", "")
+    dma("Y", T.ye[:], T.oe[:], "oe", "")
 
     lastw, readers, know, pos = {}, {}, {k: {} for k in queue}, {k: 0 for k in "VSTG"}
     for i, o in enumerate(ops):

from concourse.bass import DstId, RemoteDMATransfer
from concourse.mybir import AluOpType, ActivationFunctionType

ALU = AluOpType
ACT = ActivationFunctionType
NR, L, W, C, RO = 8, 384, 4096, 48, 3
PAD = 16
ZW = PAD + W + L
WINW = 9 * L
MAGIC = 12582912.0
EMPTY = -2048.0 + 1.0 / 1024
SSETS = [[10, 11], [12, 13], [14, 15]]
S0 = SSETS[0][0]
SPLIT = 6


def _sb(shape, dtype):
    return ("sbuf", [128] + shape, dtype)


SCRATCH = {"nt": _sb([12, 2, 16], "float16"), "eq": _sb([24, L], "bfloat16")}
for _d, _n, _names in (
        ("bfloat16", ZW, "z"), ("int32", L, "bi"), ("bfloat16", 8, "wb"), ("int32", 8, "pidx"),
        ("int32", 4, "pint"), ("float32", 32, "cols"), ("float32", 16, "tric e16"), ("int32", 176, "jw jw2"),
        ("float32", 128, "cg rc"), ("float32", 144, "cidx"), ("float32", 24, "sent0 sent wf zc zd ze zf"),
        ("bfloat16", 176, "jb njb jk nj8"), ("float32", 176, "j32k j32"), ("float16", 176, "j16 nj16 nj16k nm0 nm1"),
        ("bfloat16", 144, "bw bw10"), ("float16", 144, "bw16 bw9"), ("bfloat16", 15 * 128, "tri"), ("float16", 128, "bo16"),
        ("bfloat16", 128, "bo ug ug4 vu bc wd8 nw ku kc0 kc b2k sga sgb"), ("bfloat16", 256, "crow"),
        ("bfloat16", L, "ones a s kp zx new qs oh m oa"), ("float16", L, "n16 x16 yp y"),
        ("float32", L, "f t1 ru r2 q0 oe arr0 arr1 arr2"), ("float32", WINW, "win0 win1 win2"),
        ("uint16", L, "lst"), ("bfloat16", 16 * L, "mv"), ("bfloat16", (16 - S0) * L, "v"), ("uint16", 24, "xl sll zl")):
    for _k in _names.split():
        SCRATCH[_k] = _sb([_n], _d)
for _k in (0, 2, 3, 4, 5, 6, 7):
    SCRATCH["P%d" % _k] = ("psum", [128, 512], "float32")
SCRATCH["P1"] = ("psum", [128, 16, 2, 16], "float32")

SEMAPHORES = ["cV", "cS", "cT", "cG", "sent"] + ["arr%d" % _k for _k in range(RO)] + ["dma%d" % _k for _k in range(8)]


def send_calls(topo, cores, src):
    here = topo.chip(src)
    near = [c for c in cores if c != src and topo.chip(c) == here]
    far = sorted((c for c in cores if topo.chip(c) != here), key=lambda c: topo.mates(topo.chip(c), here))
    pool = topo.engines(src, far[0])
    calls = []
    for part in (far[:4], far[4:]):
        n = len(pool) // len(part)
        calls.append({c: pool[n * k:n * k + n] for k, c in enumerate(part)})
    for c in near:
        calls[0][c] = [e for e in topo.engines(src, c) if e not in pool]
    return calls


def rank_program(g, core, T, topo):
    q = T.rank_of(core)
    if q is None:
        return
    cores = list(T.cores)
    queue = {"V": g.vector, "S": g.scalar, "T": g.tensor, "G": g, "Y": g.sync}
    ops = []
    ndma = [0]

    def op(eng, fn, rd, wr, sem=None, val=None):
        ops.append({"q": eng, "fn": fn, "rd": rd.split(), "wr": wr.split(), "sem": sem, "val": val})

    def dma(eng, out, in_, rd, wr):
        op(eng, lambda: queue[eng].dma_start(out, in_), rd, wr, "dma%d" % ndma[0], 16)
        ndma[0] += 1

    def ts(out, in0, s1, s2, o0, o1, rd, wr):
        if o1 is None:
            op("V", lambda: g.vector.tensor_scalar(out, in0, s1, None, o0), rd, wr)
        else:
            op("V", lambda: g.vector.tensor_scalar(out, in0, s1, s2, o0, o1), rd, wr)

    def tt(out, in0, in1, o, rd, wr):
        op("V", lambda: g.vector.tensor_tensor(out, in0, in1, o), rd, wr)

    def cp(out, in_, rd, wr):
        op("V", lambda: g.vector.tensor_copy(out, in_), rd, wr)

    def ms(out, c, wr):
        op("V", lambda: g.vector.memset(out, c), "", wr)

    def tr(out, in_, rd, wr):
        op("V", lambda: g.vector.transpose(out, in_), rd, wr)

    def scan(out, d0, d1, init, o0, o1, rd, wr):
        op("V", lambda: g.vector.tensor_tensor_scan(out, d0, d1, init, o0, o1), rd, wr)

    def act(out, in_, func, bias, scale, rd, wr):
        op("S", lambda: g.scalar.activation(out, in_, func, bias=bias, scale=scale), rd, wr)

    def mm(out, lhsT, rhs, start, stop, rd, wr):
        op("T", lambda: g.tensor.matmul(out, lhsT, rhs, start, stop), rd, wr)

    def iota(out, pattern, base, cm, wr, flag=True):
        if flag:
            op("G", lambda: g.iota(out, pattern, base, cm, allow_small_or_imprecise_dtypes=True), "", wr)
        else:
            op("G", lambda: g.iota(out, pattern, base, cm), "", wr)

    def col(k):
        return T.cols[:, k:k + 1]

    def row_is(k):
        return T.e16[:, k:k + 1]

    def row_lt(k):
        return T.tric[:, k:k + 1]

    def J(buf, d):
        return buf[:, 32 - d:160 - d]

    def B(buf, p):
        return buf[:, 15 - p:143 - p]

    ID, RELU, SIGN = ACT.Identity, ACT.Relu, ACT.Sign
    MUL, ADD, SUB, EQ = ALU.mult, ALU.add, ALU.subtract, ALU.is_equal
    P0, P2, P3, P4, P5, P6, P7 = (T["P%d" % k][:, 0:L] for k in (0, 2, 3, 4, 5, 6, 7))
    P1 = T.P1[:, 0:12]
    A = T.a[:]

    dma("Y", T.bi[:], T.bills[:], "", "bi")
    dma("S", A, T.due[:], "", "a0")
    dma("Y", T.z[:, PAD:PAD + W // 2], T.z0[:, 0:W // 2], "", "z")
    dma("S", T.z[:, PAD + W // 2:PAD + W], T.z0[:, W // 2:W], "", "zB")
    dma("Y", T.wb[:, 0:1], T.wt[:], "", "wb")

    def prefill(k):
        for d in range(NR):
            ms(T["win%d" % k][:, L * d:L * d + C], EMPTY, "win%d_%d" % (k, d))

    def tri(j, eng):
        out = T.tri[:, (j - 1) * 128:j * 128]
        if eng == "V":
            ts(out, T.bc[:], row_lt(j), None, MUL, None, "bc tric", "tri%d" % j)
        else:
            act(out, T.bc[:], ID, 0.0, row_lt(j), "bc tric", "tri%d" % j)

    iota(T.pidx[:, 0:1], [[0, 1]], 0, 1, "pidx", False)
    iota(T.jw[:], [[1, 176]], 256 - 32, -1, "jw", False)
    iota(T.cg[:], [[16, 8], [0, 16]], 0, 0, "cg")
    iota(T.rc[:], [[0, 8], [1, 16]], 0, 0, "rc")
    iota(T.cidx[:], [[1, 144]], -1, 0, "cidx")
    iota(T.sent0[:], [[16, 24]], PAD + W, 0, "sent0")
    ms(T.ones[:], 1.0, "ones")
    for k, b in enumerate((15, 112, 16)):
        ts(T.pint[:, k:k + 1], T.pidx[:, 0:1], b, None, ALU.bitwise_and, None, "pidx", "pint%d" % k)
    ms(T.z[:, PAD + W:ZW], 0.0, "zC")
    ms(T.z[:, 0:PAD], 0.0, "zD")
    cp(T.cols[:, 0:3], T.pint[:, 0:3], "pint0 pint1 pint2", "c0")
    ts(T.jw2[:], T.jw[:], 127, None, ALU.bitwise_and, None, "jw", "jw2")
    ts(col(4), col(2), 0.0, -1.0, EQ, MUL, "c0", "c4")
    ts(col(5), col(2), 16.0, -1.0, EQ, MUL, "c0", "c5")
    ts(T.jb[:], T.jw2[:], 0.0, None, EQ, None, "jw2", "jb")
    ts(T.bo[:], T.cg[:], col(1), None, EQ, None, "cg c0", "bo")
    ts(T.nm0[:], T.jw2[:], 0.0, col(4), EQ, MUL, "jw2 c4", "nm0")
    ts(T.e16[:], T.rc[:, 0:16], col(0), None, EQ, None, "rc c0", "e16")
    ts(T.tric[:], T.rc[:, 0:16], col(0), None, ALU.is_gt, None, "rc c0", "tric")
    ts(T.nm1[:], T.jw2[:], 0.0, col(5), EQ, MUL, "jw2 c5", "nm1")
    op("G", lambda: g.affine_select(T.ug[:], T.bo[:], [[-1, 128]], ALU.is_ge, 0.0, 0, 1), "bo", "ug")
    act(col(6), col(1), ID, 14.0, 1.0, "c0", "c6")
    act(col(7), col(0), ID, -65536.0, 4096.0, "c0", "c7")
    act(col(11), col(0), ID, 15.0, -1.0, "c0", "c11")
    act(col(26), col(0), ID, -4092.0, -4095.0, "c0", "c26")
    act(col(27), col(0), ID, -1729.0, 384.0, "c0", "c27")
    act(T.njb[:], T.jb[:], ID, 0.0, -1.0, "jb", "njb")
    act(T.bc[:], T.bo[:], ID, 0.0, 1.0, "bo", "bc")
    act(T.jk[:], T.jb[:], ID, 0.0, 1.0 / 1024, "jb", "jk")
    act(T.bc[:, q:128:16], T.bo[:, q:128:16], ID, 0.0, -2.0, "bo", "bc")
    act(T.nj8[:], T.jb[:], ID, 0.0, -8192.0, "jb", "nj8")
    act(T.bc[:, 9:128:16], T.bo[:, 9:128:16], ID, 0.0, -1.0, "bo", "bc")
    act(col(10), row_lt(S0), ID, 3.0, -9.5, "tric", "c10")
    act(T.crow[0:1, 0:128], T.rc[0:1, :], ID, 1.4375, 0.0, "rc", "crowA")
    ts(T.bw[:], T.cidx[:], col(6), None, EQ, None, "cidx c6", "bw")
    cp(T.j16[:], T.jb[:], "jb", "j16")
    ts(T.nj16[:], T.jb[:], -1.0, None, MUL, None, "jb", "nj16")
    cp(T.bo16[:], T.bo[:], "bo", "bo16")
    ts(T.n16[:], T.bi[:], -1.0, 2047.0, MUL, ADD, "bi", "n16")
    cp(T.bw16[:], T.bw[:], "bw", "bw16")
    tr(T.nt[:], T.n16[:], "n16", "nt")
    ts(T.sent[:], T.sent0[:], col(0), None, ADD, None, "sent0 c0", "sent")
    tt(col(14), row_is(1), row_is(15), SUB, "e16", "c14")
    ts(T.wd8[:], T.bo[:], T.wb[:, 0:1], 0.125, MUL, MUL, "bo wb", "wd8")
    ms(T.crow[0:1, 8:128:16], -0.4375, "crowA")
    ts(T.ku[:], T.bo[:], col(14), -0.5, MUL, MUL, "bo c14", "ku")
    ms(T.crow[0:1, 9:128:16], 0.5625, "crowA")
    act(T.ug4[:], T.ug[:], ID, 0.0, -4096.0, "ug", "ug4")
    act(T.j32k[:], T.jb[:], ID, 0.0, 1024.0, "jb", "j32k")
    act(T.j32[:], T.jb[:], ID, 0.0, 1.0, "jb", "j32")
    act(T.b2k[:], T.bo[:], ID, 0.0, 2048.0, "bo", "b2k")
    act(T.crow[0:1, 128:256], T.rc[0:1, :], ID, -0.4375, -0.125, "rc", "crowB")
    act(T.bw10[:], T.bw[:], ID, 0.0, row_is(10), "bw e16", "bw10")
    for j in range(2, 16, 2):
        tri(j, "S")
    act(T.nw[:], T.wd8[:], ID, 0.0, -8.0, "wd8", "nw")

    def late():
        tt(T.vu[:], T.ug4[:], J(T.nj8, 0), SUB, "ug4 nj8", "vu")
        ms(T.crow[0:1, 10:128:16], 0.0625, "crowA")
        ts(T.ku[:, 8:128:16], T.bo[:, 8:128:16], col(14), 0.5, MUL, MUL, "bo c14", "ku")
        ts(T.kc0[:], J(T.jb, 1), row_lt(15), 8192.0, MUL, MUL, "jb tric", "kc0")
        ms(T.ku[:, 9:128:16], 0.0, "ku")
        ts(T.sga[:], T.bo[:], row_is(9), -16384.0, MUL, MUL, "bo e16", "sga")
        ts(T.ku[:, 10:128:16], T.bo[:, 10:128:16], row_is(0), -0.5, MUL, MUL, "bo e16", "ku")
        ts(T.sgb[:], T.bo[:], row_is(9), -2.0, MUL, MUL, "bo e16", "sgb")
        for j in range(1, 16, 2):
            tri(j, "V")

    def later():
        tt(T.kc[:], T.kc0[:], J(T.nj8, 0), ADD, "kc0 nj8", "kc")
        ts(T.bw9[:], T.bw[:], row_lt(9), None, MUL, None, "bw tric", "bw9")
        ts(T.nj16k[:], T.jb[:], -1024.0, None, MUL, None, "jb", "nj16k")

    calls = send_calls(topo, cores, core)
    arrive = sum(len(x.get(core, ())) for c in cores if c != core for x in send_calls(topo, cores, c))
    nsent = sum(len(v) for x in calls for v in x.values())

    def unpack(k):
        a = T["arr%d" % k]
        rd = "arr%d own%d" % (k, k)
        ts(T.n16[:], a[:], MAGIC, -MAGIC, ADD, ADD, rd, "n16")
        mm(P0, J(T.j32k, 16), a[:], True, False, rd + " j32k", "P0")

    def lists(*rows):
        for p in rows:
            ts(T.lst[:, 24 * p:24 * p + 24], T.P1[:, 0:12, :, p], 2047.0 + PAD, None, ADD, None, "P1", "lst%d" % p)

    def wrap(bank, name, lhs, src, rd):
        for s in range(16):
            mm(bank[:, 0:24], B(lhs, s), src[:, s:L:16], s == 0, s == 15, rd, name)

    def zwin(lst):
        return T.z[:, 0:ZW].indirect(lst)

    ZK = "z zB zC zD"

    def vgather(p):
        tt(T.mv[:, p * L:(p + 1) * L], zwin(T.lst[:, 24 * p:24 * p + 24]), A, ALU.is_ge, ZK + " a0 lst%d" % p, "mv%d" % p)

    def sgather(i):
        a, b = SSETS[i][0], SSETS[i][-1] + 1
        act(T.v[:, (a - S0) * L:(b - S0) * L], zwin(T.lst[:, 24 * a:24 * b]), ID, 0.0, 1.0,
            ZK + "".join(" lst%d" % p for p in SSETS[i]), " ".join("v%d" % p for p in SSETS[i]))

    subbank = (("P7", P7), ("P6", P6), ("P4", P4), ("P5", P5), ("P7", P7), ("P6", P6))

    def suba(p):
        name, bank = subbank[p - S0]
        mm(bank, J(T.njb, 0), A, True, False, "a0 njb", name)

    def subv(p):
        name, bank = subbank[p - S0]
        mm(bank, J(T.jb, 0), T.v[:, (p - S0) * L:(p - S0 + 1) * L], False, True, "jb v%d" % p, name)

    def sign(p):
        name, bank = subbank[p - S0]
        act(T.mv[:, p * L:(p + 1) * L], bank, SIGN, 0.5, 1.0, name, "mv%d" % p)

    def count(p):
        mm(P3, B(T.bw, p), T.mv[:, p * L:(p + 1) * L], p == 0, p == S0 - 1, "bw mv%d" % p, "P3")

    def eq(u, a, b, last=False):
        key = "eq%d_%d" % (u, a)
        ts(T.eq[:, u, a:b], T.x16[:, 16 * u + a:16 * u + b], T.wf[:, u:u + 1], None, EQ, None, "x16 wf", key)
        a = max(a, 16)
        if b > a:
            mm(T.P5[:, 16 * u + a:16 * u + b], T.bc[:], T.eq[:, u, a:b], False, last, "bc " + key, "P5")

    for rnd in range(RO):
        sh = 1 if rnd else 0
        if rnd:
            unpack(rnd - 1)
            tr(T.nt[:], T.n16[:], "n16", "nt")
            mm(P0, J(T.nj16k, 16), T.n16[:], False, True, "n16 nj16k", "P0")
        for h2 in range(2):
            for h in range(2):
                mm(T.P1[:, 0:12, h2, :], J((T.nm0, T.nm1)[h2], 16 * (h - h2 + sh)), T.nt[:, :, h, :],
                   h == 0, h == 1, "nt nm0 nm1", "P1")
        if rnd:
            act(A, P0, ID, 0.0, 1.0, "P0", "a0")
        lists(0, 10, 11, 1)
        if rnd == 0:
            lists(12, 13, 2, 14, 15, 3, 4, 5, 6, 7, 8, 9)
        lz = lists if rnd else (lambda *rows: None)
        sgather(0)
        vgather(0)
        suba(10); suba(11)
        lz(12, 13, 2)
        sgather(1)
        vgather(1)
        mm(P2, J(T.nj16, 16 * sh), T.n16[:], True, False, "n16 nj16", "P2")
        suba(12); suba(13)
        lz(14, 15, 3)
        count(0)
        vgather(2)
        subv(10); subv(11); count(1)
        lz(4, 5, 6, 7, 8, 9)
        vgather(3)
        count(2)
        mm(P0, J(T.j16, 16 * sh), T.n16[:], True, False, "n16 j16", "P0")
        mm(P0, J(T.jk, 0), A, False, False, "a0 jk", "P0")
        sign(10); sign(11)
        subv(12); subv(13); count(3)
        sgather(2)
        vgather(4)
        count(10); suba(14); count(11); suba(15); count(4)
        vgather(5)
        count(5)
        vgather(6)
        sign(12); sign(13)
        subv(14); subv(15); count(6)
        vgather(7)
        count(12); count(13); count(7)
        sign(14); sign(15)
        vgather(8)
        count(14); count(8)
        vgather(9)
        count(15); count(9)
        if rnd == 0:
            late()
        else:
            prefill(rnd)
        act(T.s[:], P3, SIGN, col(10), 1.0, "P3 c10", "s")
        mm(P2, T.vu[:], T.s[:], False, True, "vu s", "P2")
        mm(P1, T.ug[:], T.s[:], True, True, "ug s", "P1")
        mm(P4, J(T.njb, 0), A, True, False, "a0 njb", "P4")
        mm(P5, T.crow[0:1, 0:128], T.ones[0:1, :], True, False, "crowA ones", "P5")
        ts(T.yp[:], P2, col(7), -2048.0, ADD, ALU.max, "P2 c7", "yp")
        act(T.kp[:], P1, SIGN, col(11), 1.0, "P1 c11", "kp")
        act(T.f[:], A, ID, -2048.0, 1.0 / 1024, "a0", "f")
        if rnd == 0:
            later()
        mm(P6, T.bo16[:], T.yp[:], True, True, "bo16 yp", "P6")
        wrap(T.P2, "P2", T.bw16, T.yp, "bw16 yp")
        ts(T.x16[:], P6, 30720.0, None, ADD, None, "P6", "x16")
        mm(P3, T.crow[0:1, 128:256], T.ones[0:1, :], True, False, "crowB ones", "P3")
        mm(P5, T.ku[:], T.kp[:], False, False, "ku kp", "P5")
        ts(T.wf[:], T.P2[:, 0:24], 30720.0, -2047.5, ADD, ALU.max, "P2", "wf")
        ts(T.xl[:], T.P2[:, 0:24], 32767.0 + PAD, None, ADD, None, "P2", "xl")
        act(T.zx[:], zwin(T.xl[:]), ID, 0.0, 1.0, ZK + " xl", "zx")

        order = list(range(SPLIT, 12)) + list(range(SPLIT)) + list(range(12, 24))
        for i, u in enumerate(order):
            eq(u, 0, 128 if u < SPLIT else L - 16 * u)
            if i == 4:
                mm(P4, J(T.jb, 0), T.zx[:], False, True, "jb zx", "P4")
                act(T.new[:], P4, RELU, 0.0, 1.0, "P4", "new")
            if i == 19:
                mm(P3, T.wd8[:], T.new[:], False, True, "wd8 new", "P3")
        diag = " ".join("eq%d_0" % u for u in range(24))
        for j in range(1, 16):
            mm(T.P5[:, j:L:16], T.tri[:, (j - 1) * 128:j * 128], T.eq[:, :, j], False, False, diag + " tri%d" % j, "P5")
        for u in range(SPLIT):
            eq(u, 128, L - 16 * u, u == SPLIT - 1)
        ts(T.t1[:], P3, MAGIC, -MAGIC, ADD, ADD, "P3", "t1")
        tt(T.zc[:], T.wf[:], T.sent[:], SUB, "wf sent", "zc")
        tt(T.ru[:], T.t1[:], P3, SUB, "t1 P3", "ru")
        act(T.qs[:], P3, SIGN, col(26), 8.0, "P3 c26", "qs")
        mm(P7, J(T.njb, 0), T.kp[:], True, False, "njb kp", "P7")
        mm(P2, T.kc[:], T.kp[:], True, False, "kc kp", "P2")
        mm(P2, T.nw[:], T.new[:], False, False, "nw new", "P2")
        tt(T.oh[:], T.ru[:], P5, ALU.is_ge, "ru P5", "oh")
        mm(P7, T.sgb[:], T.oh[:], False, True, "sgb oh", "P7")
        mm(P2, T.b2k[:], T.qs[:], False, False, "b2k qs", "P2")
        mm(P2, T.sga[:], T.oh[:], False, True, "sga oh", "P2")
        wrap(T.P3, "P3", T.bw10, T.oh, "bw10 oh")
        ts(T.zd[:], T.zc[:], 2047.0 + PAD, None, ADD, None, "zc", "zd")
        scan(P4, T.ones[:], T.oh[:], col(27), MUL, ADD, "ones oh c27", "P4")
        act(T.m[:], P7, RELU, 0.5, 0.5, "P7", "m")
        act(T.r2[:], P2, RELU, 20479.0, 1.0, "P2", "r2")
        tt(T.y[:], T.oh[:], P4, MUL, "oh P4", "y")
        mm(P0, J(T.nj8, 0), T.m[:], False, True, "nj8 m", "P0")
        wrap(T.P6, "P6", T.bw9, T.y, "bw9 y")
        if rnd == 0:
            prefill(0)
        tt(T.ze[:], T.zd[:], T.P3[:, 0:24], MUL, "zd P3", "ze")
        tt(T.q0[:], T.f[:], P0, ALU.max, "f P0", "q0")
        tt(T.zf[:], T.sent[:], T.ze[:], ADD, "ze sent", "zf")
        ts(T.sll[:], T.P6[:, 0:24], 1728.0, None, ADD, None, "P6", "sll")
        cp(T.zl[:], T.zf[:], "zf", "zl")
        win = T["win%d" % rnd]
        wk = " ".join("win%d_%d" % (rnd, d) for d in range(NR))
        tt(win[:, 0:WINW].indirect(T.sll[:]), T.q0[:], T.r2[:], ADD, "sll q0 r2", wk)

        def send(call, k=rnd, w=win):
            trs = []
            for c, engines in call.items():
                d = cores.index(c)
                rid, pid, _ = topo.addr(c)
                trs.append(RemoteDMATransfer(
                    dst_ids=[DstId(rid=rid, pnc=pid)], dma_engine_mask=sum(1 << e for e in engines),
                    remote_sem=T.sem["arr%d" % k], src=w[:, L * d:L * d + C], dst=T["arr%d" % k][:, C * q:C * q + C]))
            g.remote_dma_fused(trs, local_sem=T.sem.sent)

        for call in calls:
            op("G", lambda c=call, f=send: f(c), wk, "", "remote", 0)
        op("X", None, "", "arr%d" % rnd, "arr%d" % rnd, arrive)
        mm(T.P7[:, 0:C], J(T.j32, -16), win[:, L * q:L * q + C], True, True, wk + " j32", "P7")
        cp(zwin(T.zl[:]), T.new[:], "zl new", ZK)
        act(T["arr%d" % rnd][:, C * q:C * q + C], T.P7[:, 0:C], ID, 0.0, 1.0, "P7", "own%d" % rnd)

    dma("Y", T.yz[:], T.z[:, PAD:PAD + W], ZK, "")
    unpack(RO - 1)
    mm(P0, J(T.nj16k, 16), T.n16[:], False, True, "n16 nj16k", "P0")
    mm(P3, J(T.nj16k, 16), T.n16[:], True, True, "n16 nj16k", "P3")
    act(T.oa[:], P0, ID, 0.0, 1.0, "P0", "oa")
    ts(T.oe[:], P3, 1.0 / 1024, 2047.0, MUL, ADD, "P3", "oe")
    dma("S", T.ya[:], T.oa[:], "oa", "")
    dma("Y", T.ye[:], T.oe[:], "oe", "")

    lastw, readers, know, pos = {}, {}, {k: {} for k in queue}, {k: 0 for k in "VSTG"}
    for i, o in enumerate(ops):
        deps = set()
        for k in o["rd"]:
            deps.update(lastw.get(k, ()))
            if k[0] == "P":
                deps.update(j for j in readers.get(k, ()) if ops[j]["q"] != o["q"])
        for k in o["wr"]:
            deps.update(lastw.get(k, ()))
            deps.update(readers.get(k, ()))
        for k in o["rd"]:
            readers.setdefault(k, []).append(i)
        for k in o["wr"]:
            lastw[k], readers[k] = [i], []
        if o["sem"] is None:
            pos[o["q"]] += 1
            o["id"] = (o["q"], pos[o["q"]])
        else:
            o["id"] = (o["sem"], 1)
        o["waits"] = []
        kn = know.get(o["q"], {})
        for j in sorted(deps, reverse=True):
            d = ops[j]
            if j == i or (d["q"] == "T" and o["q"] == "T") or kn.get(d["id"][0], 0) >= d["id"][1]:
                continue
            o["waits"].append(j)
            d["mark"] = True
            for k, v in d["clock"].items():
                kn[k] = max(kn.get(k, 0), v)
        o["clock"] = dict(kn)
        o["clock"][o["id"][0]] = o["id"][1]
    total = {k: 0 for k in "VSTG"}
    for o in ops:
        for j in o["waits"]:
            d = ops[j]
            queue[o["q"]].wait_ge(T.sem[d["sem"] or "c" + d["q"]], d["val"])
        if o["fn"] is None:
            continue
        ins = o["fn"]()
        if o["sem"] is None:
            if o.get("mark"):
                total[o["q"]] += 1
                o["val"] = total[o["q"]]
                ins.then_inc(T.sem["c" + o["q"]], 1)
        elif o["sem"] != "remote":
            ins.then_inc(T.sem[o["sem"]], 16)
    for k in "VSTG":
        if total[k]:
            g.wait_ge(T.sem["c" + k], total[k])
    g.wait_ge(T.sem.sent, RO * nsent)
    for k in range(ndma[0]):
        g.wait_ge(T.sem["dma%d" % k], 16)
